import numpy as np, ml_dtypes
CORES = [2,42,66,74,82,90,114]
N = 7
import mx_ref
BF = ml_dtypes.bfloat16
def entries(a):
    return np.ascontiguousarray(a.T).reshape(-1)
def table(e):
    return np.ascontiguousarray(np.reshape(e, (-1, 16)).T).astype(np.int32)
def cols(t, e):
    v = np.concatenate([t.reshape(128, -1, 4), np.zeros((128, 1, 4), BF)], axis=1)
    return np.ascontiguousarray(v[:, e]).reshape(128, -1)
def cut(t, i, w=512):
    return t[:, w * i:w * i + w]
def f(rng, *shape):
    return mx_ref.flush((rng.standard_normal(shape, dtype=np.float32) * np.exp2(rng.integers(-2, 3, shape[:-1] + (1,)))).astype(BF))
def wide(rng, *shape, cols=0):
    v = rng.standard_normal(shape, dtype=np.float32) * np.exp2(rng.integers(-12, 13, shape)).astype(np.float32)
    if cols: v *= np.repeat(np.exp2(rng.integers(-cols, cols + 1, shape[:-2] + (1, shape[-1] // 4))) * (rng.random(shape[:-2] + (1, shape[-1] // 4)) > 0.0625), 4, axis=-1).astype(np.float32)
    return mx_ref.flush(v.astype(BF))
T, O = 256, 1
def places(rng, dest):
    e = np.zeros((N, T), int)
    for d in range(N): e[dest == d] = d * T + rng.permutation(T)
    return np.stack([table(e[r]) for r in range(N)])
def relabel(rng):
    p = rng.permutation(N)
    if np.all((p - np.arange(N)) % N == p[0]): p[[0, 1]] = p[[1, 0]]
    return p
def setup_inputs(rng):
    e = rng.permutation(N * T).reshape(N, T)
    return {"x": f(rng, N, 128, 4 * T), "to": np.stack([table(e[r]) for r in range(N)]), "w": f(rng, N, 128, 512 * O)}
def setup_inputs_swap(rng):
    d = setup_inputs(rng); p = rng.permutation(N); dest = np.zeros((N, T), int)
    for k in range(N): dest[p[k]] = p[(k + 1) % N]
    d["to"] = places(rng, dest); return d
def setup_inputs_ones(rng):
    d = setup_inputs(rng); i = np.arange(N); n = np.ones((N, N), int); n[i, rng.permutation(N)] += T % N
    for t in range(T // N - 1): n[i, rng.permutation(N)] += N
    d["to"] = places(rng, np.stack([rng.permutation(np.repeat(i, n[r])) for r in range(N)])); return d
def setup_inputs_runs(rng):
    d = setup_inputs(rng); p = relabel(rng); s, u = rng.integers(1, N), rng.integers(0, N); g, h = rng.permutation(N), rng.permutation(N)
    n = T // N + ((g[:, None] + h) % N < T % N)
    j = (np.arange(N) + s * np.arange(N)[:, None] + u) % N
    d["to"] = places(rng, np.stack([np.repeat(p[j[r]], n[r, j[r]]) for r in range(N)])); return d
def setup_inputs_comb(rng):
    d = setup_inputs(rng); p = relabel(rng); s, u = rng.integers(1, N), rng.integers(0, N); k = rng.permutation(N); c = np.arange(T)
    d["to"] = places(rng, np.stack([p[(c + np.where(c < T - T % N, s * r + u, k[r])) % N] for r in range(N)])); return d
def setup_inputs_spread(rng):
    d = setup_inputs(rng); d["x"] = wide(rng, N, 128, 4 * T, cols=8); return d
def check_inputs(d):
    e = np.concatenate([entries(d["to"][r]) for r in range(N)])
    return [] if np.array_equal(np.sort(e), np.arange(N * T)) else ["to"]
def reference(x, to, w):
    z = np.concatenate([x[r] for r in range(N)], axis=1)
    e = np.concatenate([entries(to[r]) for r in range(N)])
    home = np.zeros(N * T, int); home[e] = np.arange(N * T)
    y = np.zeros((N, 128, O * T), np.float32)
    for d in range(N):
        v = mx_ref.quantize(cols(z, home[d * T:d * T + T]))
        for o in range(O): y[d][:, T * o:T * o + T] = mx_ref.matmul(mx_ref.quantize(np.ascontiguousarray(cut(w[d], o))), v)
    return {"y": y}

@@ -1,0 +1,311 @@
+from concourse.bass import DstId, RemoteDMATransfer
+from concourse.mybir import dt, AluOpType, ActivationFunctionType
+
+N, C = 7, 256
+P1, P2, S2 = 37, 42, 48
+L1W = 48 + 6 * P1
+U = 1024
+
+F32, BF, I32, U16, CODES, PLANE = "float32", "bfloat16", "int32", "uint16", "float8_e4m3fn_x4", "uint8"
+SCRATCH = {
+    "ip": ("sbuf", [128, 1], I32), "pa": ("sbuf", [128, 2], I32), "pf": ("sbuf", [128, 2], F32),
+    "ic": ("sbuf", [128, 16], F32), "win": ("sbuf", [128, 16], BF), "win2": ("sbuf", [128, 16], BF),
+    "wme": ("sbuf", [128, 16], F32), "zb": ("sbuf", [128, C], BF), "zf": ("sbuf", [128, C], F32),
+    "rst": ("sbuf", [128, C], BF), "cv": ("sbuf", [128, 128], F32), "cvb": ("sbuf", [128, 128], BF),
+    "ji": ("sbuf", [128, 34], F32), "jf": ("sbuf", [128, 34], F32), "jm": ("sbuf", [128, 34], I32),
+    "ja": ("sbuf", [128, 34], F32), "jb": ("sbuf", [128, 34], F32), "jc": ("sbuf", [128, 34], F32),
+    "sig": ("sbuf", [128, 34], U16), "dup": ("sbuf", [128, 34], U16), "pos": ("sbuf", [128, 48], F32),
+    "qc": ("sbuf", [128, 8], F32), "ba": ("sbuf", [128, 8], F32), "zr": ("sbuf", [128, 8], F32),
+    "tw": ("sbuf", [128, 16], I32), "td": ("sbuf", [128, 16], I32), "td16": ("sbuf", [128, 16], U16),
+    "mk": ("sbuf", [128, C], BF), "jk": ("sbuf", [128, C], BF), "cc": ("sbuf", [128, C], BF),
+    "uu": ("sbuf", [128, C], BF), "xx": ("sbuf", [128, C], BF), "xc": ("sbuf", [128, C], BF),
+    "s16": ("sbuf", [128, 8], U16), "inv": ("sbuf", [128, 272], BF), "gg": ("sbuf", [128, 544], BF),
+    "yy": ("sbuf", [128, 544], BF), "lf": ("sbuf", [128, 18], F32), "lst1": ("sbuf", [128, 18], U16),
+    "be": ("sbuf", [128, 2], F32), "cb": ("sbuf", [128, 4 * N], F32),
+    "nn": ("sbuf", [128, 8], F32), "c7i": ("sbuf", [128, 8], I32), "c7": ("sbuf", [128, 8], F32),
+    "rx": ("sbuf", [128, 8], F32), "qa": ("sbuf", [128, 8], F32), "qi": ("sbuf", [128, 8], I32),
+    "aa": ("sbuf", [128, 8], F32), "aj": ("sbuf", [128, 8], F32), "jj": ("sbuf", [128, 8], F32),
+    "gr": ("sbuf", [128, 7 * 48], F32), "gs": ("sbuf", [128, 6 * 48], F32),
+    "l2d": ("sbuf", [128, 96], F32), "l2t": ("sbuf", [128, 96], F32), "lst2": ("sbuf", [128, 22], U16),
+    "rd": ("dram", [128, 2], I32), "lr": ("dram", [N, 128, 2], I32),
+    "tr": ("sbuf", [128, 16], I32), "tr16": ("sbuf", [128, 16], U16), "trd": ("sbuf", [128, 16], I32),
+    "trd16": ("sbuf", [128, 16], U16), "mk3": ("sbuf", [128, C], F32), "kv": ("sbuf", [128, C], F32),
+    "vw": ("sbuf", [128, N * C], F32), "vl": ("sbuf", [128, C], F32),
+    "f1": ("sbuf", [128, 8], F32), "f2": ("sbuf", [128, 8], F32), "fp": ("sbuf", [128, 32], F32),
+    "ft": ("sbuf", [128, 32], F32), "w3": ("sbuf", [128, 512], F32), "y3": ("sbuf", [128, 512], F32),
+    "fo": ("sbuf", [128, 96], F32), "pk": ("sbuf", [128, 16], I32), "pq": ("sbuf", [128, 32], I32),
+    "qq": ("sbuf", [128, 32], I32), "ua": ("sbuf", [128, 16], F32), "ub": ("sbuf", [128, 16], F32),
+    "uc": ("sbuf", [128, 16], F32), "ud": ("sbuf", [128, 16], F32), "lst3": ("sbuf", [128, 16], U16),
+    "xt": ("sbuf", [128, 4 * C], BF), "wt": ("sbuf", [128, 512], BF),
+    "xq": ("sbuf", [128, C], CODES), "xs": ("sbuf", [128, C], PLANE),
+    "wq": ("sbuf", [128, 128], CODES), "ws": ("sbuf", [128, 128], PLANE),
+    "out1q": ("sbuf", [128, 240], CODES), "out1s": ("sbuf", [128, 240], PLANE),
+    "land1q": ("sbuf", [128, L1W], CODES), "land1s": ("sbuf", [128, L1W], PLANE),
+    "out2q": ("sbuf", [128, 6 * S2], CODES), "out2s": ("sbuf", [128, 6 * S2], PLANE),
+    "land2q": ("sbuf", [128, 7 * S2], CODES), "land2s": ("sbuf", [128, 7 * S2], PLANE),
+    "fq": ("sbuf", [128, C], CODES), "fs": ("sbuf", [128, C], PLANE),
+    "ps": ("psum", [128, 1024], F32), "ys": ("sbuf", [128, C], F32),
+}
+SEMAPHORES = ["ev", "es", "eg", "et",
+              "d_rd", "d_tw", "d_x", "d_w", "d_own", "d_tr", "d_vl", "d_y0", "d_y1",
+              "a_raw", "a_cnt", "a_c1", "a_s1", "a_c2", "a_s2",
+              "l_raw", "l_cnt", "l_c1", "l_s1", "l_c2", "l_s2"]
+
+
+def rank_program(g, core, T, topo):
+    me = T.rank_of(core)
+    if me is None:
+        return
+    A, AF = AluOpType, ActivationFunctionType
+    queue = {"v": g.vector, "s": g.scalar, "g": g, "t": g.tensor, "y": g.sync}
+    count = {}
+    seen = {k: {} for k in queue}
+
+    def wait(q, *deps):
+        for sem, n in deps:
+            if seen[q].get(sem, 0) < n:
+                queue[q].wait_ge(T.sem[sem], n)
+                seen[q][sem] = n
+
+    def op(q, call, *deps):
+        wait(q, *deps)
+        sem = "e" + q
+        call().then_inc(T.sem[sem], 1)
+        count[sem] = count.get(sem, 0) + 1
+        return (sem, count[sem])
+
+    def dma(q, sem, out, in_, *deps):
+        wait(q, *deps)
+        queue[q].dma_start(out, in_).then_inc(T.sem[sem], 16)
+        count[sem] = count.get(sem, 0) + 16
+        return (sem, count[sem])
+
+    V, S = g.vector, g.scalar
+
+    peers = [T.cores[(me + 1 + x) % N] for x in range(N - 1)]
+    eng = [e for e in topo.engines(core, peers[0]) if all(e in topo.engines(core, p) for p in peers)]
+    h = len(eng) // 2
+
+    def mask(es):
+        return sum(1 << e for e in es)
+
+    one = [[e] for e in eng[:h]] + [eng[h:h + 2], eng[h + 2:h + 4]]
+    two = [eng[0:2], eng[2:4]] + [[e] for e in eng[h:]]
+
+    def dst(p):
+        rid, pid, _ = topo.addr(p)
+        return DstId(rid=rid, pnc=pid)
+
+    def to_all(src, d, remote, local):
+        g.remote_dma_fused([RemoteDMATransfer(dst_ids=[dst(p) for p in peers], dma_engine_mask=mask(eng),
+                                              remote_sem=T.sem[remote], srcs=[src], dsts=[d] * len(peers))],
+                           local_sem=T.sem[local])
+
+    def to_each(srcs, dsts, masks, remote, local):
+        g.remote_dma_fused([RemoteDMATransfer(dst_ids=[dst(p)], dma_engine_mask=mask(m), remote_sem=T.sem[remote],
+                                              src=s, dst=d) for p, s, d, m in zip(peers, srcs, dsts, masks)],
+                           local_sem=T.sem[local])
+
+    rd = dma("y", "d_rd", T.rd[:], T.to[:])
+    for i in range(8):
+        tw = dma("ys"[i % 2], "d_tw", T.tw[16 * i:16 * i + 16, :], T.to[:])
+    xl = dma("y", "d_x", T.xt[:], T.x[:])
+    own = dma("s", "d_own", T.lr[me], T.to[:])
+    wl = dma("s", "d_w", T.wt[:], T.w[:])
+
+    flag = dict(allow_small_or_imprecise_dtypes=True)
+    k_ip = op("g", lambda: g.iota(T.ip[:], [[0, 1]], 0, 1))
+    k_ic = op("g", lambda: g.iota(T.ic[:], [[1, 16]], 0, 0, **flag))
+    k_ji = op("g", lambda: g.iota(T.ji[:], [[16, 17], [0, 2]], 0, 0, **flag))
+    k_cv = op("g", lambda: g.iota(T.cv[:], [[32, 8], [1, 16]], 0, 0, **flag))
+    wait("g", rd)
+    to_all(T.rd[:], T.lr[me], "a_raw", "l_raw")
+
+    k_zb = op("v", lambda: V.memset(T.zb[:], 0.0))
+    k_rst = op("v", lambda: V.memset(T.rst[:], 1.0))
+    k_inv = op("v", lambda: V.memset(T.inv[:], 0.0))
+    k_fp = op("v", lambda: V.memset(T.fp[:], 0.0))
+    k_rx = op("v", lambda: V.memset(T.rx[:], 0.0))
+    k_aj = op("v", lambda: V.memset(T.aj[:], 0.0))
+    k_pa = op("v", lambda: V.tensor_scalar(T.pa[:, 0:1], T.ip[:], 15, None, A.bitwise_and), k_ip)
+    op("v", lambda: V.tensor_scalar(T.pa[:, 1:2], T.ip[:], 16, None, A.bitwise_and))
+    k_rst = op("v", lambda: V.memset(T.rst[:, 0:C:32], 0.0), k_rst)
+    k_pf = op("v", lambda: V.tensor_copy(T.pf[:], T.pa[:]), ("ev", count["ev"] - 1))
+    p15, odd = T.pf[:, 0:1], T.pf[:, 1:2]
+    k_win2 = op("v", lambda: V.tensor_scalar(T.win2[:], T.ic[:], p15, None, A.is_lt), k_pf, k_ic)
+    k_win = op("v", lambda: V.tensor_scalar(T.win[:], T.ic[:], p15, None, A.is_equal), k_pf, k_ic)
+    k_jf = op("v", lambda: V.tensor_scalar(T.jf[:], T.ji[:], p15, None, A.add), k_ji)
+    k_cvb = op("v", lambda: V.tensor_scalar(T.cvb[:], T.cv[:], odd, None, A.add), k_cv)
+    k_jm = op("v", lambda: V.tensor_scalar(T.jm[:], T.jf[:], -18.0, 1.0 / P1, A.add, A.mult), k_jf)
+    k_ja = op("v", lambda: V.tensor_scalar(T.ja[:], T.jf[:], 7.0, 1.0, A.mult, A.add))
+    k_jb = op("v", lambda: V.tensor_scalar(T.jb[:], T.jm[:], float(1 - 7 * P1), None, A.mult), k_jm)
+    k_dup = op("v", lambda: V.tensor_copy(T.dup[:], T.jf[:]), k_jf)
+    k_jc = op("v", lambda: V.tensor_tensor(T.jc[:], T.ja[:], T.jb[:], A.add), k_jb)
+    k_wme = op("v", lambda: V.tensor_scalar(T.wme[:], T.ic[:], float(me), float(U + 1), A.is_equal, A.mult))
+    k_sig = op("v", lambda: V.tensor_copy(T.sig[:], T.jc[:]), k_jc)
+
+    k = op("v", lambda: V.tensor_scalar(T.td[:], T.tw[:], 8, None, A.arith_shift_right), tw)
+    k_td = op("v", lambda: V.tensor_copy(T.td16[:], T.td[:]), k)
+    k_b = op("s", lambda: S.activation(T.jk[:], T.win2[:].indirect(T.td16[:]), AF.Identity, accum_out=T.be[:, 0:1]),
+             k_td, k_win2)
+    k_mk = op("v", lambda: V.tensor_copy(T.mk[:], T.win[:].indirect(T.td16[:])), k_td)
+    k_cc = op("v", lambda: V.tensor_tensor_scan(T.cc[:], T.mk[:], T.zb[:], T.be[:, 0:1], A.add, A.add), k_mk, k_b)
+    k_e = op("s", lambda: S.activation(T.be[:, 1:2], T.cc[:, C - 1:C], AF.Copy), k_cc)
+    k_own = op("s", lambda: S.activation(T.cb[:, 4 * me:4 * me + 2], T.be[:], AF.Copy), k_e)
+    k_uu = op("v", lambda: V.tensor_tensor(T.uu[:], T.cc[:], T.mk[:], A.mult), k_cc)
+    k_xx = op("v", lambda: V.transpose(T.xx[:], T.uu[:]), k_uu)
+    k_xc = op("v", lambda: V.tensor_tensor_scan(T.xc[:], T.rst[:], T.xx[:], 0.0, A.mult, A.add), k_xx)
+    k_s = op("v", lambda: V.tensor_copy(T.s16[:], T.xc[:, 15:C:32]), k_xc)
+    k_sc = op("v", lambda: V.tensor_copy(T.inv[:].indirect(T.s16[:]), T.cvb[:]), k_s)
+    k_ga = op("s", lambda: S.activation(T.gg[:, 0:352], T.inv[:].indirect(T.sig[:, 0:22]), AF.Copy), k_sc, k_sig)
+    k_gb = op("v", lambda: V.tensor_copy(T.gg[:, 352:544], T.inv[:].indirect(T.sig[:, 22:34])), k_sc)
+    k_xq = op("v", lambda: V.quantize_mx(T.xq[:], T.xs[:], T.xt[:]), xl)
+    k_yy = op("v", lambda: V.transpose(T.yy[:], T.gg[:]), k_ga, k_gb)
+    k_lf = op("v", lambda: V.tensor_tensor(T.lf[:, 0:17], T.yy[:, 0:544:32], T.yy[:, 16:544:32], A.add), k_yy)
+    k_l1 = op("v", lambda: V.tensor_copy(T.lst1[:, 0:17], T.lf[:, 0:17]), k_lf)
+
+    wait("g", k_e)
+    to_all(T.be[:], T.cb[:, 4 * me:4 * me + 2], "a_cnt", "l_cnt")
+    op("g", lambda: g.iota(T.pos[:], [[1, 48]], 0, 0, **flag))
+    op("g", lambda: g.iota(T.qc[:, 0:me + 1], [[1, me + 1]], 3 - me, 0, **flag))
+    if me < N - 1:
+        op("g", lambda: g.iota(T.qc[:, me + 1:N], [[1, N - 1 - me]], 3 - (N - 1), 0, **flag))
+    if me > 0:
+        op("g", lambda: g.iota(T.ba[:, 0:me], [[-P1, me]], 48 - P1 + P1 * me, 0, **flag))
+    op("g", lambda: g.iota(T.ba[:, me:me + 1], [[0, 1]], 0, 0, **flag))
+    if me < N - 1:
+        op("g", lambda: g.iota(T.ba[:, me + 1:N], [[-P1, N - 1 - me]], 48 - P1 + P1 * (N - 1), 0, **flag))
+    k_g = op("g", lambda: g.iota(T.zr[:, 0:N], [[1, N]], 12 - me, 0, **flag))
+
+    lo, la = T.lst1[:, 2:17], T.lst1[:, 0:3]
+    u32 = dt.uint32
+    k_p1 = op("v", lambda: V.tensor_copy(T.out1q[:].bitcast(u32), T.xq[:].bitcast(u32).indirect(lo)), k_l1, k_xq)
+    k_o1 = op("s", lambda: S.activation(T.out1s[:], T.xs[:].indirect(lo), AF.Copy), k_l1, k_xq)
+    wait("g", k_p1)
+    blk = [P1 * (x + 1) - 32 for x in range(N - 1)]
+    lnd = [48 + P1 * x for x in range(N - 1)]
+    u8 = dt.uint8
+    to_each([T.out1q[:, a:a + P1].bitcast(u8) for a in blk], [T.land1q[:, a:a + P1].bitcast(u8) for a in lnd], one,
+            "a_c1", "l_c1")
+    wait("g", k_o1)
+    to_each([T.out1s[:, a:a + P1] for a in blk], [T.land1s[:, a:a + P1] for a in lnd], two, "a_s1", "l_s1")
+    k_a1 = op("v", lambda: V.tensor_copy(T.land1q[:, 0:48].bitcast(u32), T.xq[:].bitcast(u32).indirect(la)))
+    k_b1 = op("s", lambda: S.activation(T.land1s[:, 0:48], T.xs[:].indirect(la), AF.Copy))
+
+    dma("y", "d_tr", T.tr[112:128, :], T.to[:])
+    tr = dma("y", "d_tr", T.tr[0:112, :], T.lr[:], own, ("a_raw", 6 * len(eng)))
+
+    k_vw = op("v", lambda: V.memset(T.vw[:, C * me:C * me + C], -4e6))
+    k_vl = op("v", lambda: V.memset(T.vl[:], 0.0))
+    k_zf = op("v", lambda: V.memset(T.zf[:], 0.0))
+    k_wq = op("v", lambda: V.quantize_mx(T.wq[:], T.ws[:], T.wt[:]), wl)
+    bb, ee = T.cb[:, 0:4 * N:4], T.cb[:, 1:4 * N:4]
+    cn = ("a_cnt", 6 * len(eng))
+    k_n = op("v", lambda: V.tensor_tensor(T.nn[:, 0:N], ee, bb, A.subtract), cn, k_own)
+    k_q = op("v", lambda: V.tensor_tensor(T.qa[:, 0:N], bb, T.qc[:, 0:N], A.add), k_g)
+    k_f1 = op("v", lambda: V.tensor_tensor(T.f1[:, 0:N], bb, T.zr[:, 0:N], A.add))
+    k_ci = op("v", lambda: V.tensor_scalar(T.c7i[:, 0:N], T.nn[:, 0:N], 3.0, 1.0 / 7, A.add, A.mult), k_n)
+    k_qi = op("v", lambda: V.tensor_scalar(T.qi[:, 0:N], T.qa[:, 0:N], 1.0 / 7, None, A.mult), k_q)
+    k_c7 = op("v", lambda: V.tensor_copy(T.c7[:, 0:N], T.c7i[:, 0:N]), k_ci)
+    k_aa = op("v", lambda: V.tensor_tensor(T.aa[:, 0:N], T.qi[:, 0:N], T.ba[:, 0:N], A.add), k_qi)
+    k_rx = op("v", lambda: V.tensor_tensor_scan(T.rx[:, 1:8], T.c7[:, 0:N], T.zf[:, 0:N], 0.0, A.add, A.add),
+              k_c7, k_zf, k_rx)
+    k_a = op("v", lambda: V.tensor_tensor(T.aj[:, 1:8], T.aa[:, 0:N], T.rx[:, 0:N], A.subtract), k_rx, k_aa)
+    k_f2 = op("v", lambda: V.tensor_scalar(T.f2[:, 0:N], T.rx[:, 0:N], 7.0 * U, -1.0 * U, A.mult, A.add))
+    k_jj = op("v", lambda: V.tensor_tensor(T.jj[:, 0:N], T.aj[:, 1:8], T.aj[:, 0:N], A.subtract), k_a)
+    k_f = op("v", lambda: V.tensor_tensor(T.fp[:, 0:N], T.f1[:, 0:N], T.f2[:, 0:N], A.add), k_f2)
+
+    def gr(r):
+        return T.gr[:, 48 * r:48 * r + 48]
+
+    def gs(i):
+        return T.gs[:, 48 * i:48 * i + 48]
+
+    terms = [op("v", lambda: V.tensor_scalar(gr(0), T.pos[:], T.jj[:, 0:1], None, A.add), k_jj)]
+    for r in range(1, N):
+        terms.append(op("v", lambda: V.tensor_scalar(gr(r), T.pos[:], T.rx[:, r:r + 1], T.jj[:, r:r + 1],
+                                                     A.is_ge, A.mult)))
+    k_ft = op("v", lambda: V.transpose(T.ft[:], T.fp[:]), k_f)
+    s0 = op("v", lambda: V.tensor_tensor(gs(0), gr(0), gr(1), A.add), terms[1])
+    s1 = op("v", lambda: V.tensor_tensor(gs(1), gr(2), gr(3), A.add), terms[3])
+    s2 = op("v", lambda: V.tensor_tensor(gs(2), gr(4), gr(5), A.add), terms[5])
+    s3 = op("v", lambda: V.tensor_tensor(gs(3), gs(0), gs(1), A.add), s1)
+    s4 = op("v", lambda: V.tensor_tensor(gs(4), gs(2), gr(6), A.add), s2, terms[6])
+    s5 = op("v", lambda: V.tensor_tensor(gs(5), gs(3), gs(4), A.add), s4)
+    k = op("v", lambda: V.tensor_scalar(T.l2d[:], T.gs[:, 240:288].indirect(T.dup[:, 0:6]), float(L1W - 1), None,
+                                        A.min), s5, k_dup)
+    k = op("v", lambda: V.transpose(T.l2t[:], T.l2d[:]), k)
+    for i in range(3):
+        if me < N - 1:
+            k_l2 = op("v", lambda: V.tensor_copy(T.lst2[:, i:3 * (N - 1 - me):3],
+                                                 T.l2t[:, 32 * i + me + 1:32 * i + N]), k)
+        k_l2 = op("v", lambda: V.tensor_copy(T.lst2[:, 3 * (N - 1 - me) + i:21:3],
+                                             T.l2t[:, 32 * i:32 * i + me + 1]), k)
+
+    ka = op("v", lambda: V.tensor_scalar(T.trd[:], T.tr[:], 8, None, A.arith_shift_right), tr)
+    kb = op("v", lambda: V.tensor_copy(T.tr16[:], T.tr[:]))
+    k = op("v", lambda: V.tensor_copy(T.trd16[:], T.trd[:]), ka)
+    k = op("v", lambda: V.tensor_copy(T.mk3[:], T.wme[:].indirect(T.trd16[:])), k)
+    k = op("v", lambda: V.tensor_tensor_scan(T.kv[:], T.mk3[:], T.zf[:], 0.0, A.add, A.add), k)
+    k_v = op("v", lambda: V.tensor_copy(T.vw[:].indirect(T.tr16[:]), T.kv[:]), k, kb, k_vw)
+    for i in range(4):
+        vl = dma("y", "d_vl", T.vl[32 * i:32 * i + N, :], T.vw[0:16 * N:16, C * me:C * me + C], k_v, k_vl)
+
+    lo, la = T.lst2[:, 0:18], T.lst2[:, 18:21]
+    c1, s1 = ("a_c1", 8), ("a_s1", 8)
+    k_p2 = op("v", lambda: V.tensor_copy(T.out2q[:].bitcast(u32), T.land1q[:].bitcast(u32).indirect(lo)),
+              k_l2, k_a1, c1)
+    k_o2 = op("s", lambda: S.activation(T.out2s[:], T.land1s[:].indirect(lo), AF.Copy), k_l2, k_b1, s1)
+    wait("g", k_p2)
+    blk = [S2 * x for x in range(N - 1)]
+    lnd = [S2 * (N - 2 - x) for x in range(N - 1)]
+    to_each([T.out2q[:, a:a + P2].bitcast(u8) for a in blk], [T.land2q[:, a:a + P2].bitcast(u8) for a in lnd], one,
+            "a_c2", "l_c2")
+    wait("g", k_o2)
+    to_each([T.out2s[:, a:a + P2] for a in blk], [T.land2s[:, a:a + P2] for a in lnd], two, "a_s2", "l_s2")
+    k_a2 = op("v", lambda: V.tensor_copy(T.land2q[:, 6 * S2:7 * S2].bitcast(u32),
+                                         T.land1q[:].bitcast(u32).indirect(la)))
+    k_b2 = op("s", lambda: S.activation(T.land2s[:, 6 * S2:7 * S2], T.land1s[:].indirect(la), AF.Copy))
+
+    k = op("s", lambda: S.activation(T.w3[:], T.vl[:].indirect(T.dup[:, 0:32]), AF.Relu, bias=T.ft[:, me:me + 1]),
+           vl, k_ft, k_dup)
+    k = op("v", lambda: V.transpose(T.y3[:], T.w3[:]), k)
+
+    def col(r):
+        return T.y3[:, r:512:32]
+
+    def fo(i):
+        return T.fo[:, 16 * i:16 * i + 16]
+
+    f0 = op("v", lambda: V.tensor_tensor(fo(0), col(0), col(1), A.add), k)
+    f1 = op("v", lambda: V.tensor_tensor(fo(1), col(2), col(3), A.add))
+    f2 = op("v", lambda: V.tensor_tensor(fo(2), col(4), col(5), A.add))
+    f3 = op("v", lambda: V.tensor_tensor(fo(3), fo(0), fo(1), A.add), f1)
+    f4 = op("v", lambda: V.tensor_tensor(fo(4), fo(2), col(6), A.add), f2)
+    k = op("v", lambda: V.tensor_tensor(T.pk[:], fo(3), fo(4), A.add), f4)
+    op("v", lambda: V.tensor_scalar(T.pq[:, 0:16], T.pk[:], U - 1, None, A.bitwise_and), k)
+    k = op("v", lambda: V.tensor_scalar(T.pq[:, 16:32], T.pk[:], 10, None, A.arith_shift_right))
+    k1 = op("v", lambda: V.tensor_scalar(T.qq[:], T.pq[:], -3.0, 1.0 / 7, A.add, A.mult), k)
+    k2 = op("v", lambda: V.tensor_scalar(T.ua[:], T.pq[:, 0:16], float(S2), None, A.mult))
+    k3 = op("v", lambda: V.tensor_scalar(T.ub[:], T.qq[:, 0:16], -7.0 * S2, None, A.mult), k1)
+    k4 = op("v", lambda: V.tensor_tensor(T.uc[:], T.ua[:], T.qq[:, 16:32], A.add), k2)
+    k5 = op("v", lambda: V.tensor_tensor(T.ud[:], T.ub[:], T.uc[:], A.add), k4)
+    k_l3 = op("v", lambda: V.tensor_copy(T.lst3[:], T.ud[:]), k5)
+
+    c2, s2 = ("a_c2", 8), ("a_s2", 8)
+    mm = []
+    for i in range(2):
+        cols, lst = slice(128 * i, 128 * i + 128), T.lst3[:, 8 * i:8 * i + 8]
+        kq = op("v", lambda: V.tensor_copy(T.fq[:, cols].bitcast(u32), T.land2q[:].bitcast(u32).indirect(lst)),
+                k_l3, k_a2, c2)
+        ks = op("s", lambda: S.activation(T.fs[:, cols], T.land2s[:].indirect(lst), AF.Copy), k_l3, k_b2, s2)
+        mm.append(op("t", lambda: g.tensor.matmul_mx(T.ps[:, 512 * i:512 * i + 128], T.wq[:], T.ws[:], T.fq[:, cols],
+                                                     T.fs[:, cols], True, True), kq, ks, k_wq))
+    k0 = op("v", lambda: V.tensor_copy(T.ys[:, 0:128], T.ps[:, 0:128]), mm[0])
+    k1 = op("s", lambda: S.activation(T.ys[:, 128:256], T.ps[:, 512:640], AF.Copy), mm[1])
+    y0 = dma("y", "d_y0", T.y[:, 0:128], T.ys[:, 0:128], k0)
+    y1 = dma("s", "d_y1", T.y[:, 128:256], T.ys[:, 128:256], k1)
+
+    for sem in ("l_raw", "l_cnt", "l_c1", "l_s1", "l_c2", "l_s2"):
+        wait("g", (sem, len(eng)))
+    wait("y", y0, y1, *[(s, count[s]) for s in ("ev", "es", "eg", "et")])

@@ -5,36 +5,40 @@ N, C = 7, 256
 P1, P2, S2 = 37, 42, 48
 L1W = 48 + 6 * P1
 U = 1024
+CA = 352
 
 F32, BF, I32, U16, CODES, PLANE = "float32", "bfloat16", "int32", "uint16", "float8_e4m3fn_x4", "uint8"
 SCRATCH = {
     "ip": ("sbuf", [128, 1], I32), "pa": ("sbuf", [128, 2], I32), "pf": ("sbuf", [128, 2], F32),
+    "ta": ("sbuf", [128, 65], F32), "td3": ("sbuf", [128, 64], F32),
     "ic": ("sbuf", [128, 16], F32), "win": ("sbuf", [128, 16], BF), "win2": ("sbuf", [128, 16], BF),
-    "wme": ("sbuf", [128, 16], F32), "zb": ("sbuf", [128, C], BF), "zf": ("sbuf", [128, C], F32),
-    "rst": ("sbuf", [128, C], BF), "cv": ("sbuf", [128, 128], F32), "cvb": ("sbuf", [128, 128], BF),
+    "wme": ("sbuf", [128, 16], BF), "rst": ("sbuf", [128, C], BF), "rst7": ("sbuf", [128, 7 * 32], F32),
+    "cv": ("sbuf", [128, 128], F32), "cvb": ("sbuf", [128, 128], BF),
     "ji": ("sbuf", [128, 34], F32), "jf": ("sbuf", [128, 34], F32), "jm": ("sbuf", [128, 34], I32),
     "ja": ("sbuf", [128, 34], F32), "jb": ("sbuf", [128, 34], F32), "jc": ("sbuf", [128, 34], F32),
-    "sig": ("sbuf", [128, 34], U16), "dup": ("sbuf", [128, 34], U16), "pos": ("sbuf", [128, 48], F32),
+    "sig": ("sbuf", [128, 34], U16), "dup": ("sbuf", [128, 34], U16), "pos": ("sbuf", [128, 32], F32),
     "qc": ("sbuf", [128, 8], F32), "ba": ("sbuf", [128, 8], F32), "zr": ("sbuf", [128, 8], F32),
     "tw": ("sbuf", [128, 16], I32), "td": ("sbuf", [128, 16], I32), "td16": ("sbuf", [128, 16], U16),
-    "mk": ("sbuf", [128, C], BF), "jk": ("sbuf", [128, C], BF), "cc": ("sbuf", [128, C], BF),
-    "uu": ("sbuf", [128, C], BF), "xx": ("sbuf", [128, C], BF), "xc": ("sbuf", [128, C], BF),
+    "mk": ("sbuf", [128, C], BF), "jk": ("sbuf", [128, C], BF), "jn": ("sbuf", [128, C], BF),
+    "dm": ("sbuf", [128, C], BF), "cc": ("sbuf", [128, C], BF),
+    "xx": ("sbuf", [128, C], BF), "xc": ("sbuf", [128, C], BF),
     "s16": ("sbuf", [128, 8], U16), "inv": ("sbuf", [128, 272], BF), "gg": ("sbuf", [128, 544], BF),
     "yy": ("sbuf", [128, 544], BF), "lf": ("sbuf", [128, 18], F32), "lst1": ("sbuf", [128, 18], U16),
-    "be": ("sbuf", [128, 2], F32), "cb": ("sbuf", [128, 4 * N], F32),
-    "nn": ("sbuf", [128, 8], F32), "c7i": ("sbuf", [128, 8], I32), "c7": ("sbuf", [128, 8], F32),
+    "cb": ("sbuf", [128, 4 * N], F32),
+    "c7i": ("sbuf", [128, 8], I32), "c7": ("sbuf", [128, 8], F32),
     "rx": ("sbuf", [128, 8], F32), "qa": ("sbuf", [128, 8], F32), "qi": ("sbuf", [128, 8], I32),
     "aa": ("sbuf", [128, 8], F32), "aj": ("sbuf", [128, 8], F32), "jj": ("sbuf", [128, 8], F32),
-    "gr": ("sbuf", [128, 7 * 48], F32), "gs": ("sbuf", [128, 6 * 48], F32),
-    "l2d": ("sbuf", [128, 96], F32), "l2t": ("sbuf", [128, 96], F32), "lst2": ("sbuf", [128, 22], U16),
+    "gr": ("sbuf", [128, 7 * 32], F32), "gs": ("sbuf", [128, 7 * 32], F32),
+    "l2t": ("sbuf", [128, 32], F32), "lst2": ("sbuf", [128, 22], U16),
     "rd": ("dram", [128, 2], I32), "lr": ("dram", [N, 128, 2], I32),
     "tr": ("sbuf", [128, 16], I32), "tr16": ("sbuf", [128, 16], U16), "trd": ("sbuf", [128, 16], I32),
-    "trd16": ("sbuf", [128, 16], U16), "mk3": ("sbuf", [128, C], F32), "kv": ("sbuf", [128, C], F32),
-    "vw": ("sbuf", [128, N * C], F32), "vl": ("sbuf", [128, C], F32),
+    "trd16": ("sbuf", [128, 16], U16), "mk3": ("sbuf", [128, C], BF), "kv": ("sbuf", [128, C], BF),
+    "vw": ("sbuf", [128, N * C], BF), "vl": ("sbuf", [128, C], BF),
     "f1": ("sbuf", [128, 8], F32), "f2": ("sbuf", [128, 8], F32), "fp": ("sbuf", [128, 32], F32),
     "ft": ("sbuf", [128, 32], F32), "w3": ("sbuf", [128, 512], F32), "y3": ("sbuf", [128, 512], F32),
-    "fo": ("sbuf", [128, 96], F32), "pk": ("sbuf", [128, 16], I32), "pq": ("sbuf", [128, 32], I32),
-    "qq": ("sbuf", [128, 32], I32), "ua": ("sbuf", [128, 16], F32), "ub": ("sbuf", [128, 16], F32),
+    "fa": ("sbuf", [128, 64], F32), "fb": ("sbuf", [128, 32], F32), "pk": ("sbuf", [128, 16], I32),
+    "ql": ("sbuf", [128, 16], I32), "qh": ("sbuf", [128, 16], I32), "qq": ("sbuf", [128, 16], I32),
+    "ua": ("sbuf", [128, 16], F32), "ub": ("sbuf", [128, 16], F32),
     "uc": ("sbuf", [128, 16], F32), "ud": ("sbuf", [128, 16], F32), "lst3": ("sbuf", [128, 16], U16),
     "xt": ("sbuf", [128, 4 * C], BF), "wt": ("sbuf", [128, 512], BF),
     "xq": ("sbuf", [128, C], CODES), "xs": ("sbuf", [128, C], PLANE),
@@ -84,20 +88,20 @@ def rank_program(g, core, T, topo):
 
     peers = [T.cores[(me + 1 + x) % N] for x in range(N - 1)]
     eng = [e for e in topo.engines(core, peers[0]) if all(e in topo.engines(core, p) for p in peers)]
-    h = len(eng) // 2
+    ev, od = eng[0::2], eng[1::2]
 
     def mask(es):
         return sum(1 << e for e in es)
 
-    one = [[e] for e in eng[:h]] + [eng[h:h + 2], eng[h + 2:h + 4]]
-    two = [eng[0:2], eng[2:4]] + [[e] for e in eng[h:]]
+    one = [[e] for e in ev] + [od[0:2], od[2:4]]
+    two = [ev[0:2], ev[2:4]] + [[e] for e in od]
 
     def dst(p):
         rid, pid, _ = topo.addr(p)
         return DstId(rid=rid, pnc=pid)
 
-    def to_all(src, d, remote, local):
-        g.remote_dma_fused([RemoteDMATransfer(dst_ids=[dst(p) for p in peers], dma_engine_mask=mask(eng),
+    def to_all(src, d, es, remote, local):
+        g.remote_dma_fused([RemoteDMATransfer(dst_ids=[dst(p) for p in peers], dma_engine_mask=mask(es),
                                               remote_sem=T.sem[remote], srcs=[src], dsts=[d] * len(peers))],
                            local_sem=T.sem[local])
 
@@ -108,83 +112,74 @@ def rank_program(g, core, T, topo):
 
     rd = dma("y", "d_rd", T.rd[:], T.to[:])
     for i in range(8):
-        tw = dma("ys"[i % 2], "d_tw", T.tw[16 * i:16 * i + 16, :], T.to[:])
+        tw = dma("sy"[i % 2], "d_tw", T.tw[16 * i:16 * i + 16, :], T.to[:])
     xl = dma("y", "d_x", T.xt[:], T.x[:])
     own = dma("s", "d_own", T.lr[me], T.to[:])
     wl = dma("s", "d_w", T.wt[:], T.w[:])
 
     flag = dict(allow_small_or_imprecise_dtypes=True)
+    k = op("g", lambda: g.iota(T.ta[:, 0:33], [[1, 11], [0, 3]], 0, 0, **flag))
+    k_ta = op("g", lambda: g.iota(T.ta[:, 32:65], [[0, 11], [16, 3]], 0, 0, **flag), k)
     k_ip = op("g", lambda: g.iota(T.ip[:], [[0, 1]], 0, 1))
     k_ic = op("g", lambda: g.iota(T.ic[:], [[1, 16]], 0, 0, **flag))
     k_ji = op("g", lambda: g.iota(T.ji[:], [[16, 17], [0, 2]], 0, 0, **flag))
     k_cv = op("g", lambda: g.iota(T.cv[:], [[32, 8], [1, 16]], 0, 0, **flag))
     wait("g", rd)
-    to_all(T.rd[:], T.lr[me], "a_raw", "l_raw")
+    raw = eng[:1]
+    to_all(T.rd[:], T.lr[me], raw, "a_raw", "l_raw")
 
-    k_zb = op("v", lambda: V.memset(T.zb[:], 0.0))
+    op("v", lambda: V.memset(T.dm[:, 0:1], -255.0))
     k_rst = op("v", lambda: V.memset(T.rst[:], 1.0))
     k_inv = op("v", lambda: V.memset(T.inv[:], 0.0))
-    k_fp = op("v", lambda: V.memset(T.fp[:], 0.0))
-    k_rx = op("v", lambda: V.memset(T.rx[:], 0.0))
-    k_aj = op("v", lambda: V.memset(T.aj[:], 0.0))
-    k_pa = op("v", lambda: V.tensor_scalar(T.pa[:, 0:1], T.ip[:], 15, None, A.bitwise_and), k_ip)
-    op("v", lambda: V.tensor_scalar(T.pa[:, 1:2], T.ip[:], 16, None, A.bitwise_and))
-    k_rst = op("v", lambda: V.memset(T.rst[:, 0:C:32], 0.0), k_rst)
-    k_pf = op("v", lambda: V.tensor_copy(T.pf[:], T.pa[:]), ("ev", count["ev"] - 1))
+    op("v", lambda: V.memset(T.fp[:], 0.0))
+    op("v", lambda: V.memset(T.rx[:, 0:1], 0.0))
+    op("v", lambda: V.memset(T.aj[:, 0:1], 0.0))
+    k_mem = op("v", lambda: V.memset(T.rst[:, 0:C:32], 0.0), k_rst)
+    k_td3 = op("v", lambda: V.transpose(T.td3[:], T.ta[:, 0:64]), k_ta)
+    pd, pr = T.td3[:, 0:1], T.td3[:, 32:33]
+    op("v", lambda: V.tensor_scalar(T.pa[:, 0:1], T.ip[:], 15, None, A.bitwise_and), k_ip)
+    k_pa = op("v", lambda: V.tensor_scalar(T.pa[:, 1:2], T.ip[:], 16, None, A.bitwise_and))
+    k_win2 = op("v", lambda: V.tensor_scalar(T.win2[:], T.ic[:], pd, None, A.is_lt), k_td3, k_ic)
+    k_win = op("v", lambda: V.tensor_scalar(T.win[:], T.ic[:], pd, 256.0, A.is_equal, A.mult))
+    k_pf = op("v", lambda: V.tensor_copy(T.pf[:], T.pa[:]), k_pa)
     p15, odd = T.pf[:, 0:1], T.pf[:, 1:2]
-    k_win2 = op("v", lambda: V.tensor_scalar(T.win2[:], T.ic[:], p15, None, A.is_lt), k_pf, k_ic)
-    k_win = op("v", lambda: V.tensor_scalar(T.win[:], T.ic[:], p15, None, A.is_equal), k_pf, k_ic)
-    k_jf = op("v", lambda: V.tensor_scalar(T.jf[:], T.ji[:], p15, None, A.add), k_ji)
-    k_cvb = op("v", lambda: V.tensor_scalar(T.cvb[:], T.cv[:], odd, None, A.add), k_cv)
+    k_jf = op("s", lambda: S.activation(T.jf[:], T.ji[:], AF.Identity, bias=p15), k_pf, k_ji)
+    k_ja = op("s", lambda: S.activation(T.ja[:], T.jf[:], AF.Identity, bias=1.0, scale=7.0), k_jf)
+    k_cvb = op("s", lambda: S.activation(T.cvb[:], T.cv[:], AF.Identity, bias=odd), k_cv)
     k_jm = op("v", lambda: V.tensor_scalar(T.jm[:], T.jf[:], -18.0, 1.0 / P1, A.add, A.mult), k_jf)
-    k_ja = op("v", lambda: V.tensor_scalar(T.ja[:], T.jf[:], 7.0, 1.0, A.mult, A.add))
     k_jb = op("v", lambda: V.tensor_scalar(T.jb[:], T.jm[:], float(1 - 7 * P1), None, A.mult), k_jm)
-    k_dup = op("v", lambda: V.tensor_copy(T.dup[:], T.jf[:]), k_jf)
-    k_jc = op("v", lambda: V.tensor_tensor(T.jc[:], T.ja[:], T.jb[:], A.add), k_jb)
-    k_wme = op("v", lambda: V.tensor_scalar(T.wme[:], T.ic[:], float(me), float(U + 1), A.is_equal, A.mult))
+    k_jc = op("v", lambda: V.tensor_tensor(T.jc[:], T.ja[:], T.jb[:], A.add), k_jb, k_ja)
     k_sig = op("v", lambda: V.tensor_copy(T.sig[:], T.jc[:]), k_jc)
 
     k = op("v", lambda: V.tensor_scalar(T.td[:], T.tw[:], 8, None, A.arith_shift_right), tw)
     k_td = op("v", lambda: V.tensor_copy(T.td16[:], T.td[:]), k)
-    k_b = op("s", lambda: S.activation(T.jk[:], T.win2[:].indirect(T.td16[:]), AF.Identity, accum_out=T.be[:, 0:1]),
-             k_td, k_win2)
-    k_mk = op("v", lambda: V.tensor_copy(T.mk[:], T.win[:].indirect(T.td16[:])), k_td)
-    k_cc = op("v", lambda: V.tensor_tensor_scan(T.cc[:], T.mk[:], T.zb[:], T.be[:, 0:1], A.add, A.add), k_mk, k_b)
-    k_e = op("s", lambda: S.activation(T.be[:, 1:2], T.cc[:, C - 1:C], AF.Copy), k_cc)
-    k_own = op("s", lambda: S.activation(T.cb[:, 4 * me:4 * me + 2], T.be[:], AF.Copy), k_e)
-    k_uu = op("v", lambda: V.tensor_tensor(T.uu[:], T.cc[:], T.mk[:], A.mult), k_cc)
-    k_xx = op("v", lambda: V.transpose(T.xx[:], T.uu[:]), k_uu)
-    k_xc = op("v", lambda: V.tensor_tensor_scan(T.xc[:], T.rst[:], T.xx[:], 0.0, A.mult, A.add), k_xx)
-    k_s = op("v", lambda: V.tensor_copy(T.s16[:], T.xc[:, 15:C:32]), k_xc)
-    k_sc = op("v", lambda: V.tensor_copy(T.inv[:].indirect(T.s16[:]), T.cvb[:]), k_s)
-    k_ga = op("s", lambda: S.activation(T.gg[:, 0:352], T.inv[:].indirect(T.sig[:, 0:22]), AF.Copy), k_sc, k_sig)
-    k_gb = op("v", lambda: V.tensor_copy(T.gg[:, 352:544], T.inv[:].indirect(T.sig[:, 22:34])), k_sc)
+    bm, nm = T.cb[:, 4 * me:4 * me + 1], T.cb[:, 4 * me + 1:4 * me + 2]
+    k_b = op("s", lambda: S.activation(T.jk[:], T.win2[:].indirect(T.td16[:]), AF.Identity, accum_out=bm), k_td, k_win2)
+    k_mk = op("v", lambda: V.tensor_copy(T.mk[:], T.win[:].indirect(T.td16[:])), k_td, k_win)
+    k_nm = op("s", lambda: S.activation(T.jn[:], T.mk[:], AF.Copy, scale=1.0 / 256, accum_out=nm), k_mk)
+    k_dm = op("v", lambda: V.tensor_scalar(T.dm[:, 1:C], T.mk[:, 0:C - 1], -255.0 / 256, None, A.mult), k_mk)
+    k_cc = op("v", lambda: V.tensor_tensor_scan(T.cc[:], T.mk[:], T.dm[:], bm, A.add, A.add), k_dm, k_b)
+    k_xx = op("v", lambda: V.transpose(T.xx[:], T.cc[:]), k_cc)
+    k_xc = op("v", lambda: V.tensor_tensor_scan(T.xc[:], T.rst[:], T.xx[:], 0.0, A.mult, A.max), k_xx, k_mem)
+    k_s = op("v", lambda: V.tensor_copy(T.s16[:], T.xc[:, 31:C:32]), k_xc)
+    k_sc = op("v", lambda: V.tensor_copy(T.inv[:].indirect(T.s16[:]), T.cvb[:]), k_s, k_cvb, k_inv)
+    k_ga = op("s", lambda: S.activation(T.gg[:, 0:CA], T.inv[:].indirect(T.sig[:, 0:CA // 16]), AF.Copy), k_sc, k_sig)
+    k_gb = op("v", lambda: V.tensor_copy(T.gg[:, CA:544], T.inv[:].indirect(T.sig[:, CA // 16:34])), k_sc)
     k_xq = op("v", lambda: V.quantize_mx(T.xq[:], T.xs[:], T.xt[:]), xl)
     k_yy = op("v", lambda: V.transpose(T.yy[:], T.gg[:]), k_ga, k_gb)
     k_lf = op("v", lambda: V.tensor_tensor(T.lf[:, 0:17], T.yy[:, 0:544:32], T.yy[:, 16:544:32], A.add), k_yy)
     k_l1 = op("v", lambda: V.tensor_copy(T.lst1[:, 0:17], T.lf[:, 0:17]), k_lf)
 
-    wait("g", k_e)
-    to_all(T.be[:], T.cb[:, 4 * me:4 * me + 2], "a_cnt", "l_cnt")
-    op("g", lambda: g.iota(T.pos[:], [[1, 48]], 0, 0, **flag))
-    op("g", lambda: g.iota(T.qc[:, 0:me + 1], [[1, me + 1]], 3 - me, 0, **flag))
-    if me < N - 1:
-        op("g", lambda: g.iota(T.qc[:, me + 1:N], [[1, N - 1 - me]], 3 - (N - 1), 0, **flag))
-    if me > 0:
-        op("g", lambda: g.iota(T.ba[:, 0:me], [[-P1, me]], 48 - P1 + P1 * me, 0, **flag))
-    op("g", lambda: g.iota(T.ba[:, me:me + 1], [[0, 1]], 0, 0, **flag))
-    if me < N - 1:
-        op("g", lambda: g.iota(T.ba[:, me + 1:N], [[-P1, N - 1 - me]], 48 - P1 + P1 * (N - 1), 0, **flag))
-    k_g = op("g", lambda: g.iota(T.zr[:, 0:N], [[1, N]], 12 - me, 0, **flag))
+    wait("g", k_nm)
+    to_all(T.cb[:, 4 * me:4 * me + 2], T.cb[:, 4 * me:4 * me + 2], eng, "a_cnt", "l_cnt")
 
     lo, la = T.lst1[:, 2:17], T.lst1[:, 0:3]
-    u32 = dt.uint32
+    u32, u8 = dt.uint32, dt.uint8
     k_p1 = op("v", lambda: V.tensor_copy(T.out1q[:].bitcast(u32), T.xq[:].bitcast(u32).indirect(lo)), k_l1, k_xq)
     k_o1 = op("s", lambda: S.activation(T.out1s[:], T.xs[:].indirect(lo), AF.Copy), k_l1, k_xq)
     wait("g", k_p1)
     blk = [P1 * (x + 1) - 32 for x in range(N - 1)]
     lnd = [48 + P1 * x for x in range(N - 1)]
-    u8 = dt.uint8
     to_each([T.out1q[:, a:a + P1].bitcast(u8) for a in blk], [T.land1q[:, a:a + P1].bitcast(u8) for a in lnd], one,
             "a_c1", "l_c1")
     wait("g", k_o1)
@@ -192,64 +187,60 @@ def rank_program(g, core, T, topo):
     k_a1 = op("v", lambda: V.tensor_copy(T.land1q[:, 0:48].bitcast(u32), T.xq[:].bitcast(u32).indirect(la)))
     k_b1 = op("s", lambda: S.activation(T.land1s[:, 0:48], T.xs[:].indirect(la), AF.Copy))
 
+    op("g", lambda: g.iota(T.vw[:, C * me:C * me + C], [[0, C]], -4096, 0, **flag))
+    k_vl = op("g", lambda: g.iota(T.vl[:], [[0, C]], 0, 0, **flag))
+
     dma("y", "d_tr", T.tr[112:128, :], T.to[:])
-    tr = dma("y", "d_tr", T.tr[0:112, :], T.lr[:], own, ("a_raw", 6 * len(eng)))
+    tr = dma("y", "d_tr", T.tr[0:112, :], T.lr[:], own, ("a_raw", 6 * len(raw)))
 
-    k_vw = op("v", lambda: V.memset(T.vw[:, C * me:C * me + C], -4e6))
-    k_vl = op("v", lambda: V.memset(T.vl[:], 0.0))
-    k_zf = op("v", lambda: V.memset(T.zf[:], 0.0))
-    k_wq = op("v", lambda: V.quantize_mx(T.wq[:], T.ws[:], T.wt[:]), wl)
-    bb, ee = T.cb[:, 0:4 * N:4], T.cb[:, 1:4 * N:4]
+    def lin(out, a, b, scale, bias):
+        return op("s", lambda: S.activation(out[:, a:b], T.ic[:, a:b], AF.Identity, bias=float(bias), scale=float(scale)),
+                  k_ic)
+
+    lin(T.qc, 0, me + 1, 1, 3 - me)
+    if me < N - 1:
+        lin(T.qc, me + 1, N, 1, 3 - me - N)
+        lin(T.ba, me + 1, N, -P1, 48 - P1 + P1 * (me + N))
+    if me > 0:
+        lin(T.ba, 0, me, -P1, 48 - P1 + P1 * me)
+    lin(T.ba, me, me + 1, 0, 0)
+    op("s", lambda: S.activation(T.pos[:, 0:16], T.ic[:], AF.Identity, bias=pr), k_td3)
+    k_pos = op("s", lambda: S.activation(T.pos[:, 16:32], T.ic[:], AF.Identity, bias=pr))
+    k_zr = lin(T.zr, 0, N, 1, 12 - me)
+
+    k_r7 = op("v", lambda: V.memset(T.rst7[:], 1.0))
+    k_r7 = op("v", lambda: V.memset(T.rst7[:, 0:224:7], 0.0), k_r7)
+    k_wme = op("v", lambda: V.tensor_scalar(T.wme[:], T.ic[:], float(me), None, A.is_equal))
+    k_dup = op("v", lambda: V.tensor_copy(T.dup[:], T.jf[:]))
+    bb, nn = T.cb[:, 0:4 * N:4], T.cb[:, 1:4 * N:4]
     cn = ("a_cnt", 6 * len(eng))
-    k_n = op("v", lambda: V.tensor_tensor(T.nn[:, 0:N], ee, bb, A.subtract), cn, k_own)
-    k_q = op("v", lambda: V.tensor_tensor(T.qa[:, 0:N], bb, T.qc[:, 0:N], A.add), k_g)
-    k_f1 = op("v", lambda: V.tensor_tensor(T.f1[:, 0:N], bb, T.zr[:, 0:N], A.add))
-    k_ci = op("v", lambda: V.tensor_scalar(T.c7i[:, 0:N], T.nn[:, 0:N], 3.0, 1.0 / 7, A.add, A.mult), k_n)
-    k_qi = op("v", lambda: V.tensor_scalar(T.qi[:, 0:N], T.qa[:, 0:N], 1.0 / 7, None, A.mult), k_q)
+    k_ci = op("v", lambda: V.tensor_scalar(T.c7i[:, 0:N], nn, 3.0, 1.0 / 7, A.add, A.mult), cn, k_nm)
+    k_q = op("v", lambda: V.tensor_tensor(T.qa[:, 0:N], bb, T.qc[:, 0:N], A.add), k_pos)
     k_c7 = op("v", lambda: V.tensor_copy(T.c7[:, 0:N], T.c7i[:, 0:N]), k_ci)
+    k_qi = op("v", lambda: V.tensor_scalar(T.qi[:, 0:N], T.qa[:, 0:N], 1.0 / 7, None, A.mult), k_q)
+    k_rx = op("v", lambda: V.tensor_tensor_scan(T.rx[:, 1:8], T.c7[:, 0:N], T.c7[:, 0:N], 0.0, A.add, A.max), k_c7)
     k_aa = op("v", lambda: V.tensor_tensor(T.aa[:, 0:N], T.qi[:, 0:N], T.ba[:, 0:N], A.add), k_qi)
-    k_rx = op("v", lambda: V.tensor_tensor_scan(T.rx[:, 1:8], T.c7[:, 0:N], T.zf[:, 0:N], 0.0, A.add, A.add),
-              k_c7, k_zf, k_rx)
     k_a = op("v", lambda: V.tensor_tensor(T.aj[:, 1:8], T.aa[:, 0:N], T.rx[:, 0:N], A.subtract), k_rx, k_aa)
-    k_f2 = op("v", lambda: V.tensor_scalar(T.f2[:, 0:N], T.rx[:, 0:N], 7.0 * U, -1.0 * U, A.mult, A.add))
     k_jj = op("v", lambda: V.tensor_tensor(T.jj[:, 0:N], T.aj[:, 1:8], T.aj[:, 0:N], A.subtract), k_a)
-    k_f = op("v", lambda: V.tensor_tensor(T.fp[:, 0:N], T.f1[:, 0:N], T.f2[:, 0:N], A.add), k_f2)
-
-    def gr(r):
-        return T.gr[:, 48 * r:48 * r + 48]
-
-    def gs(i):
-        return T.gs[:, 48 * i:48 * i + 48]
-
-    terms = [op("v", lambda: V.tensor_scalar(gr(0), T.pos[:], T.jj[:, 0:1], None, A.add), k_jj)]
-    for r in range(1, N):
-        terms.append(op("v", lambda: V.tensor_scalar(gr(r), T.pos[:], T.rx[:, r:r + 1], T.jj[:, r:r + 1],
-                                                     A.is_ge, A.mult)))
-    k_ft = op("v", lambda: V.transpose(T.ft[:], T.fp[:]), k_f)
-    s0 = op("v", lambda: V.tensor_tensor(gs(0), gr(0), gr(1), A.add), terms[1])
-    s1 = op("v", lambda: V.tensor_tensor(gs(1), gr(2), gr(3), A.add), terms[3])
-    s2 = op("v", lambda: V.tensor_tensor(gs(2), gr(4), gr(5), A.add), terms[5])
-    s3 = op("v", lambda: V.tensor_tensor(gs(3), gs(0), gs(1), A.add), s1)
-    s4 = op("v", lambda: V.tensor_tensor(gs(4), gs(2), gr(6), A.add), s2, terms[6])
-    s5 = op("v", lambda: V.tensor_tensor(gs(5), gs(3), gs(4), A.add), s4)
-    k = op("v", lambda: V.tensor_scalar(T.l2d[:], T.gs[:, 240:288].indirect(T.dup[:, 0:6]), float(L1W - 1), None,
-                                        A.min), s5, k_dup)
-    k = op("v", lambda: V.transpose(T.l2t[:], T.l2d[:]), k)
-    for i in range(3):
-        if me < N - 1:
-            k_l2 = op("v", lambda: V.tensor_copy(T.lst2[:, i:3 * (N - 1 - me):3],
-                                                 T.l2t[:, 32 * i + me + 1:32 * i + N]), k)
-        k_l2 = op("v", lambda: V.tensor_copy(T.lst2[:, 3 * (N - 1 - me) + i:21:3],
-                                             T.l2t[:, 32 * i:32 * i + me + 1]), k)
-
     ka = op("v", lambda: V.tensor_scalar(T.trd[:], T.tr[:], 8, None, A.arith_shift_right), tr)
     kb = op("v", lambda: V.tensor_copy(T.tr16[:], T.tr[:]))
-    k = op("v", lambda: V.tensor_copy(T.trd16[:], T.trd[:]), ka)
-    k = op("v", lambda: V.tensor_copy(T.mk3[:], T.wme[:].indirect(T.trd16[:])), k)
-    k = op("v", lambda: V.tensor_tensor_scan(T.kv[:], T.mk3[:], T.zf[:], 0.0, A.add, A.add), k)
-    k_v = op("v", lambda: V.tensor_copy(T.vw[:].indirect(T.tr16[:]), T.kv[:]), k, kb, k_vw)
+    k_t3 = op("v", lambda: V.tensor_copy(T.trd16[:], T.trd[:]), ka)
+    k_mk3 = op("s", lambda: S.activation(T.mk3[:], T.wme[:].indirect(T.trd16[:]), AF.Copy), k_t3, k_wme)
+    k_gr = op("v", lambda: V.tensor_scalar(T.gr[:, 0:224:7], T.pos[:], T.jj[:, 0:1], None, A.add), k_jj)
+    for r in range(1, N):
+        k_gr = op("v", lambda: V.tensor_scalar(T.gr[:, r:224:7], T.pos[:], T.rx[:, r:r + 1], T.jj[:, r:r + 1],
+                                               A.is_ge, A.mult))
+    k = op("v", lambda: V.tensor_tensor_scan(T.gs[:], T.rst7[:], T.gr[:], 0.0, A.mult, A.add), k_gr, k_r7)
+    k = op("v", lambda: V.transpose(T.l2t[:], T.gs[:, 6:224:7]), k)
+    e = 3 * (N - 1 - me)
+    if e:
+        op("v", lambda: V.tensor_scalar(T.lst2[:, 0:e], T.l2t[:, 3 * (me + 1):21], float(L1W - 1), None, A.min), k)
+    k_l2 = op("v", lambda: V.tensor_scalar(T.lst2[:, e:21], T.l2t[:, 0:3 * (me + 1)], float(L1W - 1), None, A.min), k)
+
+    k = op("v", lambda: V.tensor_tensor_scan(T.kv[:], T.mk3[:], T.mk3[:], 0.0, A.add, A.max), k_mk3)
+    k_v = op("v", lambda: V.tensor_copy(T.vw[:].indirect(T.tr16[:]), T.kv[:]), k, kb, k_vl)
     for i in range(4):
-        vl = dma("y", "d_vl", T.vl[32 * i:32 * i + N, :], T.vw[0:16 * N:16, C * me:C * me + C], k_v, k_vl)
+        vl = dma("y", "d_vl", T.vl[32 * i:32 * i + 4 * N:4, :], T.vw[0:16 * N:16, C * me:C * me + C], k_v, k_vl)
 
     lo, la = T.lst2[:, 0:18], T.lst2[:, 18:21]
     c1, s1 = ("a_c1", 8), ("a_s1", 8)
@@ -266,46 +257,44 @@ def rank_program(g, core, T, topo):
     k_a2 = op("v", lambda: V.tensor_copy(T.land2q[:, 6 * S2:7 * S2].bitcast(u32),
                                          T.land1q[:].bitcast(u32).indirect(la)))
     k_b2 = op("s", lambda: S.activation(T.land2s[:, 6 * S2:7 * S2], T.land1s[:].indirect(la), AF.Copy))
+    k_f1 = op("v", lambda: V.tensor_tensor(T.f1[:, 0:N], bb, T.zr[:, 0:N], A.add), k_zr)
+    k_f2 = op("v", lambda: V.tensor_scalar(T.f2[:, 0:N], T.rx[:, 0:N], 7.0 * U, -1.0 * U, A.mult, A.add))
+    k_f = op("v", lambda: V.tensor_tensor(T.fp[:, 0:4 * N:4], T.f1[:, 0:N], T.f2[:, 0:N], A.add), k_f2)
+    k_ft = op("v", lambda: V.transpose(T.ft[:], T.fp[:]), k_f)
+    k_wq = op("v", lambda: V.quantize_mx(T.wq[:], T.ws[:], T.wt[:]), wl)
 
-    k = op("s", lambda: S.activation(T.w3[:], T.vl[:].indirect(T.dup[:, 0:32]), AF.Relu, bias=T.ft[:, me:me + 1]),
-           vl, k_ft, k_dup)
-    k = op("v", lambda: V.transpose(T.y3[:], T.w3[:]), k)
-
-    def col(r):
-        return T.y3[:, r:512:32]
-
-    def fo(i):
-        return T.fo[:, 16 * i:16 * i + 16]
-
-    f0 = op("v", lambda: V.tensor_tensor(fo(0), col(0), col(1), A.add), k)
-    f1 = op("v", lambda: V.tensor_tensor(fo(1), col(2), col(3), A.add))
-    f2 = op("v", lambda: V.tensor_tensor(fo(2), col(4), col(5), A.add))
-    f3 = op("v", lambda: V.tensor_tensor(fo(3), fo(0), fo(1), A.add), f1)
-    f4 = op("v", lambda: V.tensor_tensor(fo(4), fo(2), col(6), A.add), f2)
-    k = op("v", lambda: V.tensor_tensor(T.pk[:], fo(3), fo(4), A.add), f4)
-    op("v", lambda: V.tensor_scalar(T.pq[:, 0:16], T.pk[:], U - 1, None, A.bitwise_and), k)
-    k = op("v", lambda: V.tensor_scalar(T.pq[:, 16:32], T.pk[:], 10, None, A.arith_shift_right))
-    k1 = op("v", lambda: V.tensor_scalar(T.qq[:], T.pq[:], -3.0, 1.0 / 7, A.add, A.mult), k)
-    k2 = op("v", lambda: V.tensor_scalar(T.ua[:], T.pq[:, 0:16], float(S2), None, A.mult))
-    k3 = op("v", lambda: V.tensor_scalar(T.ub[:], T.qq[:, 0:16], -7.0 * S2, None, A.mult), k1)
-    k4 = op("v", lambda: V.tensor_tensor(T.uc[:], T.ua[:], T.qq[:, 16:32], A.add), k2)
-    k5 = op("v", lambda: V.tensor_tensor(T.ud[:], T.ub[:], T.uc[:], A.add), k4)
-    k_l3 = op("v", lambda: V.tensor_copy(T.lst3[:], T.ud[:]), k5)
+    for i in range(2):
+        h = slice(256 * i, 256 * i + 256)
+        k = op("s", lambda: S.activation(T.w3[:, h], T.vl[:].indirect(T.dup[:, 16 * i:16 * i + 16]), AF.Relu,
+                                         bias=T.ft[:, 3 * me:3 * me + 1], scale=float(U + 1)), vl, k_ft, k_dup)
+        k = op("v", lambda: V.transpose(T.y3[:, h], T.w3[:, h]), k)
+    k = op("v", lambda: V.tensor_tensor(T.fa[:], T.y3[:, 0:512:8], T.y3[:, 4:512:8], A.add), k)
+    k = op("v", lambda: V.tensor_tensor(T.fb[:], T.fa[:, 0:64:2], T.fa[:, 1:64:2], A.add), k)
+    k = op("v", lambda: V.tensor_tensor(T.pk[:], T.fb[:, 0:32:2], T.fb[:, 1:32:2], A.add), k)
+    kl = op("v", lambda: V.tensor_scalar(T.ql[:], T.pk[:], U - 1, None, A.bitwise_and), k)
+    kh = op("v", lambda: V.tensor_scalar(T.qh[:], T.pk[:], 0.5 - 3.5 * U, 1.0 / (7 * U), A.add, A.mult))
+    kq = op("v", lambda: V.tensor_scalar(T.qq[:], T.ql[:], -3.0, 1.0 / 7, A.add, A.mult), kl)
+    ka = op("v", lambda: V.tensor_scalar(T.ua[:], T.ql[:], float(S2), None, A.mult))
+    kb = op("v", lambda: V.tensor_scalar(T.ub[:], T.qq[:], -7.0 * S2, None, A.mult), kq)
+    kc = op("v", lambda: V.tensor_tensor(T.uc[:], T.ua[:], T.qh[:], A.add), ka, kh)
+    kd = op("v", lambda: V.tensor_tensor(T.ud[:], T.ub[:], T.uc[:], A.add), kb, kc)
+    k_l3 = op("v", lambda: V.tensor_copy(T.lst3[:], T.ud[:]), kd)
 
     c2, s2 = ("a_c2", 8), ("a_s2", 8)
-    mm = []
-    for i in range(2):
-        cols, lst = slice(128 * i, 128 * i + 128), T.lst3[:, 8 * i:8 * i + 8]
-        kq = op("v", lambda: V.tensor_copy(T.fq[:, cols].bitcast(u32), T.land2q[:].bitcast(u32).indirect(lst)),
-                k_l3, k_a2, c2)
-        ks = op("s", lambda: S.activation(T.fs[:, cols], T.land2s[:].indirect(lst), AF.Copy), k_l3, k_b2, s2)
-        mm.append(op("t", lambda: g.tensor.matmul_mx(T.ps[:, 512 * i:512 * i + 128], T.wq[:], T.ws[:], T.fq[:, cols],
-                                                     T.fs[:, cols], True, True), kq, ks, k_wq))
-    k0 = op("v", lambda: V.tensor_copy(T.ys[:, 0:128], T.ps[:, 0:128]), mm[0])
-    k1 = op("s", lambda: S.activation(T.ys[:, 128:256], T.ps[:, 512:640], AF.Copy), mm[1])
-    y0 = dma("y", "d_y0", T.y[:, 0:128], T.ys[:, 0:128], k0)
-    y1 = dma("s", "d_y1", T.y[:, 128:256], T.ys[:, 128:256], k1)
+    cols = [slice(128 * i, 128 * i + 128) for i in range(2)]
+    lst = [T.lst3[:, 8 * i:8 * i + 8] for i in range(2)]
+    kq = [op("v", lambda: V.tensor_copy(T.fq[:, cols[i]].bitcast(u32), T.land2q[:].bitcast(u32).indirect(lst[i])),
+             k_l3, k_a2, c2) for i in range(2)]
+    ks = [op("s", lambda: S.activation(T.fs[:, cols[0]], T.land2s[:].indirect(lst[0]), AF.Copy), k_l3, k_b2, s2),
+          op("v", lambda: V.tensor_copy(T.fs[:, cols[1]], T.land2s[:].indirect(lst[1])), k_b2, s2)]
+    mm = [op("t", lambda: g.tensor.matmul_mx(T.ps[:, 512 * i:512 * i + 128], T.wq[:], T.ws[:], T.fq[:, cols[i]],
+                                             T.fs[:, cols[i]], True, True), kq[i], ks[i], k_wq) for i in range(2)]
+    k0 = op("s", lambda: S.activation(T.ys[:, 0:128], T.ps[:, 0:128], AF.Copy), mm[0])
+    k1 = op("v", lambda: V.tensor_copy(T.ys[:, 128:256], T.ps[:, 512:640]), mm[1])
+    y0 = dma("s", "d_y0", T.y[:, 0:128], T.ys[:, 0:128], k0)
+    y1 = dma("y", "d_y1", T.y[:, 128:256], T.ys[:, 128:256], k1)
 
-    for sem in ("l_raw", "l_cnt", "l_c1", "l_s1", "l_c2", "l_s2"):
+    wait("g", ("l_raw", len(raw)))
+    for sem in ("l_cnt", "l_c1", "l_s1", "l_c2", "l_s2"):
         wait("g", (sem, len(eng)))
     wait("y", y0, y1, *[(s, count[s]) for s in ("ev", "es", "eg", "et")])

@@ -6,35 +6,37 @@ P1, P2, S2 = 37, 42, 48
 L1W = 48 + 6 * P1
 U = 1024
 CA = 352
+R23 = 12582912.0
 
 F32, BF, I32, U16, CODES, PLANE = "float32", "bfloat16", "int32", "uint16", "float8_e4m3fn_x4", "uint8"
 SCRATCH = {
-    "ip": ("sbuf", [128, 1], I32), "pa": ("sbuf", [128, 2], I32), "pf": ("sbuf", [128, 2], F32),
-    "ta": ("sbuf", [128, 65], F32), "td3": ("sbuf", [128, 64], F32),
-    "ic": ("sbuf", [128, 16], F32), "win": ("sbuf", [128, 16], BF), "win2": ("sbuf", [128, 16], BF),
+    "ta": ("sbuf", [128, 33], F32), "td3": ("sbuf", [128, 32], F32),
+    "tb": ("sbuf", [128, 65], F32), "tdb": ("sbuf", [128, 64], F32), "tdc": ("sbuf", [128, 32], F32),
+    "ic": ("sbuf", [128, 32], F32), "win": ("sbuf", [128, 16], BF), "win2": ("sbuf", [128, 16], BF),
     "wme": ("sbuf", [128, 16], BF), "rst": ("sbuf", [128, C], BF), "rst7": ("sbuf", [128, 7 * 32], F32),
     "cv": ("sbuf", [128, 128], F32), "cvb": ("sbuf", [128, 128], BF),
-    "ji": ("sbuf", [128, 34], F32), "jf": ("sbuf", [128, 34], F32), "jm": ("sbuf", [128, 34], I32),
+    "ji": ("sbuf", [128, 34], F32), "jm": ("sbuf", [128, 34], I32), "jf": ("sbuf", [128, 34], F32),
     "ja": ("sbuf", [128, 34], F32), "jb": ("sbuf", [128, 34], F32), "jc": ("sbuf", [128, 34], F32),
-    "sig": ("sbuf", [128, 34], U16), "dup": ("sbuf", [128, 34], U16), "pos": ("sbuf", [128, 32], F32),
+    "sig": ("sbuf", [128, 34], U16), "dup": ("sbuf", [128, 32], U16), "pos": ("sbuf", [128, 32], F32),
     "qc": ("sbuf", [128, 8], F32), "ba": ("sbuf", [128, 8], F32), "zr": ("sbuf", [128, 8], F32),
-    "tw": ("sbuf", [128, 16], I32), "td": ("sbuf", [128, 16], I32), "td16": ("sbuf", [128, 16], U16),
-    "mk": ("sbuf", [128, C], BF), "jk": ("sbuf", [128, C], BF), "jn": ("sbuf", [128, C], BF),
+    "mg": ("sbuf", [128, 8], F32),
+    "tw": ("sbuf", [128, 16], I32), "td16": ("sbuf", [128, 16], U16),
+    "mk": ("sbuf", [128, C], BF), "jk": ("sbuf", [128, C], BF), "jn": ("sbuf", [128, C], F32),
     "dm": ("sbuf", [128, C], BF), "cc": ("sbuf", [128, C], BF),
     "xx": ("sbuf", [128, C], BF), "xc": ("sbuf", [128, C], BF),
     "s16": ("sbuf", [128, 8], U16), "inv": ("sbuf", [128, 272], BF), "gg": ("sbuf", [128, 544], BF),
     "yy": ("sbuf", [128, 544], BF), "lf": ("sbuf", [128, 18], F32), "lst1": ("sbuf", [128, 18], U16),
-    "cb": ("sbuf", [128, 4 * N], F32),
-    "c7i": ("sbuf", [128, 8], I32), "c7": ("sbuf", [128, 8], F32),
-    "rx": ("sbuf", [128, 8], F32), "qa": ("sbuf", [128, 8], F32), "qi": ("sbuf", [128, 8], I32),
-    "aa": ("sbuf", [128, 8], F32), "aj": ("sbuf", [128, 8], F32), "jj": ("sbuf", [128, 8], F32),
+    "cb": ("sbuf", [128, 4 * N], F32), "c7": ("sbuf", [128, 8], F32),
+    "zz": ("sbuf", [128, 48], F32),
+    "qa": ("sbuf", [128, 8], F32), "qi": ("sbuf", [128, 8], I32),
+    "aa": ("sbuf", [128, 8], F32), "jj": ("sbuf", [128, 8], F32),
     "gr": ("sbuf", [128, 7 * 32], F32), "gs": ("sbuf", [128, 7 * 32], F32),
     "l2t": ("sbuf", [128, 32], F32), "lst2": ("sbuf", [128, 22], U16),
     "rd": ("dram", [128, 2], I32), "lr": ("dram", [N, 128, 2], I32),
-    "tr": ("sbuf", [128, 16], I32), "tr16": ("sbuf", [128, 16], U16), "trd": ("sbuf", [128, 16], I32),
+    "tr": ("sbuf", [128, 16], I32), "tr16": ("sbuf", [128, 16], U16),
     "trd16": ("sbuf", [128, 16], U16), "mk3": ("sbuf", [128, C], BF), "kv": ("sbuf", [128, C], BF),
     "vw": ("sbuf", [128, N * C], BF), "vl": ("sbuf", [128, C], BF),
-    "f1": ("sbuf", [128, 8], F32), "f2": ("sbuf", [128, 8], F32), "fp": ("sbuf", [128, 32], F32),
+    "f1": ("sbuf", [128, 8], F32), "f2": ("sbuf", [128, 8], F32),
     "ft": ("sbuf", [128, 32], F32), "w3": ("sbuf", [128, 512], F32), "y3": ("sbuf", [128, 512], F32),
     "fa": ("sbuf", [128, 64], F32), "fb": ("sbuf", [128, 32], F32), "pk": ("sbuf", [128, 16], I32),
     "ql": ("sbuf", [128, 16], I32), "qh": ("sbuf", [128, 16], I32), "qq": ("sbuf", [128, 16], I32),
@@ -118,57 +120,68 @@ def rank_program(g, core, T, topo):
     wl = dma("s", "d_w", T.wt[:], T.w[:])
 
     flag = dict(allow_small_or_imprecise_dtypes=True)
-    k = op("g", lambda: g.iota(T.ta[:, 0:33], [[1, 11], [0, 3]], 0, 0, **flag))
-    k_ta = op("g", lambda: g.iota(T.ta[:, 32:65], [[0, 11], [16, 3]], 0, 0, **flag), k)
-    k_ip = op("g", lambda: g.iota(T.ip[:], [[0, 1]], 0, 1))
-    k_ic = op("g", lambda: g.iota(T.ic[:], [[1, 16]], 0, 0, **flag))
+    k_ta = op("g", lambda: g.iota(T.ta[:], [[1, 11], [0, 3]], 0, 0, **flag))
+    k_ic = op("g", lambda: g.iota(T.ic[:], [[0, 2], [1, 16]], 0, 0, **flag))
     k_ji = op("g", lambda: g.iota(T.ji[:], [[16, 17], [0, 2]], 0, 0, **flag))
+    k_tb = op("g", lambda: g.iota(T.tb[:, 0:32], [[16, 2], [0, 16]], 0, 0, **flag))
     k_cv = op("g", lambda: g.iota(T.cv[:], [[32, 8], [1, 16]], 0, 0, **flag))
     wait("g", rd)
     raw = eng[:1]
     to_all(T.rd[:], T.lr[me], raw, "a_raw", "l_raw")
+    k_tc = op("g", lambda: g.iota(T.tb[:, 32:65], [[0, 11], [16, 3]], 0, 0, **flag))
 
     op("v", lambda: V.memset(T.dm[:, 0:1], -255.0))
     k_rst = op("v", lambda: V.memset(T.rst[:], 1.0))
     k_inv = op("v", lambda: V.memset(T.inv[:], 0.0))
-    op("v", lambda: V.memset(T.fp[:], 0.0))
-    op("v", lambda: V.memset(T.rx[:, 0:1], 0.0))
-    op("v", lambda: V.memset(T.aj[:, 0:1], 0.0))
+    k_td3 = op("v", lambda: V.transpose(T.td3[:], T.ta[:, 0:32]), k_ta)
     k_mem = op("v", lambda: V.memset(T.rst[:, 0:C:32], 0.0), k_rst)
-    k_td3 = op("v", lambda: V.transpose(T.td3[:], T.ta[:, 0:64]), k_ta)
-    pd, pr = T.td3[:, 0:1], T.td3[:, 32:33]
-    op("v", lambda: V.tensor_scalar(T.pa[:, 0:1], T.ip[:], 15, None, A.bitwise_and), k_ip)
-    k_pa = op("v", lambda: V.tensor_scalar(T.pa[:, 1:2], T.ip[:], 16, None, A.bitwise_and))
-    k_win2 = op("v", lambda: V.tensor_scalar(T.win2[:], T.ic[:], pd, None, A.is_lt), k_td3, k_ic)
-    k_win = op("v", lambda: V.tensor_scalar(T.win[:], T.ic[:], pd, 256.0, A.is_equal, A.mult))
-    k_pf = op("v", lambda: V.tensor_copy(T.pf[:], T.pa[:]), k_pa)
-    p15, odd = T.pf[:, 0:1], T.pf[:, 1:2]
-    k_jf = op("s", lambda: S.activation(T.jf[:], T.ji[:], AF.Identity, bias=p15), k_pf, k_ji)
-    k_ja = op("s", lambda: S.activation(T.ja[:], T.jf[:], AF.Identity, bias=1.0, scale=7.0), k_jf)
-    k_cvb = op("s", lambda: S.activation(T.cvb[:], T.cv[:], AF.Identity, bias=odd), k_cv)
+    pd, p15, odd, pr = T.td3[:, 0:1], T.tdc[:, 0:1], T.tdb[:, 0:1], T.tdb[:, 32:33]
+    k_win2 = op("v", lambda: V.tensor_scalar(T.win2[:], T.ic[:, 0:16], pd, None, A.is_lt), k_td3, k_ic)
+    k_win = op("v", lambda: V.tensor_scalar(T.win[:], T.ic[:, 0:16], pd, 256.0, A.is_equal, A.mult))
+    k_tdc = op("v", lambda: V.transpose(T.tdc[:], T.ic[:]))
+    k_wme = op("v", lambda: V.tensor_scalar(T.wme[:], T.ic[:, 0:16], float(me), None, A.is_equal))
+    k_tdb = op("v", lambda: V.transpose(T.tdb[:, 0:32], T.tb[:, 0:32]), k_tb)
+    k_jf = op("s", lambda: S.activation(T.jf[:], T.ji[:], AF.Identity, bias=p15), k_tdc, k_ji)
     k_jm = op("v", lambda: V.tensor_scalar(T.jm[:], T.jf[:], -18.0, 1.0 / P1, A.add, A.mult), k_jf)
-    k_jb = op("v", lambda: V.tensor_scalar(T.jb[:], T.jm[:], float(1 - 7 * P1), None, A.mult), k_jm)
-    k_jc = op("v", lambda: V.tensor_tensor(T.jc[:], T.ja[:], T.jb[:], A.add), k_jb, k_ja)
-    k_sig = op("v", lambda: V.tensor_copy(T.sig[:], T.jc[:]), k_jc)
+    k_ja = op("s", lambda: S.activation(T.ja[:], T.jf[:], AF.Identity, bias=1.0, scale=7.0), k_jf)
 
-    k = op("v", lambda: V.tensor_scalar(T.td[:], T.tw[:], 8, None, A.arith_shift_right), tw)
-    k_td = op("v", lambda: V.tensor_copy(T.td16[:], T.td[:]), k)
+    k_td = op("v", lambda: V.tensor_scalar(T.td16[:], T.tw[:], -127.5, 1.0 / C, A.add, A.mult), tw)
     bm, nm = T.cb[:, 4 * me:4 * me + 1], T.cb[:, 4 * me + 1:4 * me + 2]
     k_b = op("s", lambda: S.activation(T.jk[:], T.win2[:].indirect(T.td16[:]), AF.Identity, accum_out=bm), k_td, k_win2)
+    k_jb = op("v", lambda: V.tensor_scalar(T.jb[:], T.jm[:], float(1 - 7 * P1), None, A.mult), k_jm)
     k_mk = op("v", lambda: V.tensor_copy(T.mk[:], T.win[:].indirect(T.td16[:])), k_td, k_win)
-    k_nm = op("s", lambda: S.activation(T.jn[:], T.mk[:], AF.Copy, scale=1.0 / 256, accum_out=nm), k_mk)
+    k_nm = op("s", lambda: S.activation(T.jn[:], T.mk[:], AF.Identity, bias=3.0 / 7 / C, scale=1.0 / 7 / 256,
+                                        accum_out=nm), k_mk)
+    k_jc = op("v", lambda: V.tensor_tensor(T.jc[:], T.ja[:], T.jb[:], A.add), k_jb, k_ja)
     k_dm = op("v", lambda: V.tensor_scalar(T.dm[:, 1:C], T.mk[:, 0:C - 1], -255.0 / 256, None, A.mult), k_mk)
+    k_sig = op("v", lambda: V.tensor_copy(T.sig[:], T.jc[:]), k_jc)
     k_cc = op("v", lambda: V.tensor_tensor_scan(T.cc[:], T.mk[:], T.dm[:], bm, A.add, A.add), k_dm, k_b)
     k_xx = op("v", lambda: V.transpose(T.xx[:], T.cc[:]), k_cc)
     k_xc = op("v", lambda: V.tensor_tensor_scan(T.xc[:], T.rst[:], T.xx[:], 0.0, A.mult, A.max), k_xx, k_mem)
     k_s = op("v", lambda: V.tensor_copy(T.s16[:], T.xc[:, 31:C:32]), k_xc)
+    k_cvb = op("s", lambda: S.activation(T.cvb[:], T.cv[:], AF.Identity, bias=odd), k_cv, k_tdb)
     k_sc = op("v", lambda: V.tensor_copy(T.inv[:].indirect(T.s16[:]), T.cvb[:]), k_s, k_cvb, k_inv)
+
+    def lin(out, a, b, scale, bias):
+        return op("s", lambda: S.activation(out[:, a:b], T.ic[:, a:b], AF.Identity, bias=float(bias), scale=float(scale)),
+                  k_ic)
+
+    fp, rx, aj = T.zz[:, 0:32], 32, 40
+    k_zz = op("s", lambda: S.activation(T.zz[:], T.cv[:, 0:48], AF.Copy, scale=0.0))
+    k_mg = lin(T.mg, 0, 8, 0, -R23)
+    op("s", lambda: S.activation(T.rst7[:, 0:128], T.cv[:], AF.Identity, bias=1.0, scale=0.0))
+    k_r7 = op("s", lambda: S.activation(T.rst7[:, 128:224], T.cv[:, 0:96], AF.Identity, bias=1.0, scale=0.0))
+    k_r7 = op("s", lambda: S.activation(T.rst7[:, 0:224:7], T.cv[:, 0:32], AF.Copy, scale=0.0), k_r7)
+
     k_ga = op("s", lambda: S.activation(T.gg[:, 0:CA], T.inv[:].indirect(T.sig[:, 0:CA // 16]), AF.Copy), k_sc, k_sig)
-    k_gb = op("v", lambda: V.tensor_copy(T.gg[:, CA:544], T.inv[:].indirect(T.sig[:, CA // 16:34])), k_sc)
+    k_gb = op("v", lambda: V.tensor_copy(T.gg[:, CA:544], T.inv[:].indirect(T.sig[:, CA // 16:34])), k_sc, k_sig)
     k_xq = op("v", lambda: V.quantize_mx(T.xq[:], T.xs[:], T.xt[:]), xl)
     k_yy = op("v", lambda: V.transpose(T.yy[:], T.gg[:]), k_ga, k_gb)
     k_lf = op("v", lambda: V.tensor_tensor(T.lf[:, 0:17], T.yy[:, 0:544:32], T.yy[:, 16:544:32], A.add), k_yy)
     k_l1 = op("v", lambda: V.tensor_copy(T.lst1[:, 0:17], T.lf[:, 0:17]), k_lf)
+    k_qc = lin(T.qc, 0, me + 1, 1, 3 - me)
+    if me < N - 1:
+        k_qc = lin(T.qc, me + 1, N, 1, 3 - me - N)
 
     wait("g", k_nm)
     to_all(T.cb[:, 4 * me:4 * me + 2], T.cb[:, 4 * me:4 * me + 2], eng, "a_cnt", "l_cnt")
@@ -185,50 +198,41 @@ def rank_program(g, core, T, topo):
     wait("g", k_o1)
     to_each([T.out1s[:, a:a + P1] for a in blk], [T.land1s[:, a:a + P1] for a in lnd], two, "a_s1", "l_s1")
     k_a1 = op("v", lambda: V.tensor_copy(T.land1q[:, 0:48].bitcast(u32), T.xq[:].bitcast(u32).indirect(la)))
+    k_tdd = op("v", lambda: V.transpose(T.tdb[:, 32:64], T.tb[:, 32:64]), k_tc)
     k_b1 = op("s", lambda: S.activation(T.land1s[:, 0:48], T.xs[:].indirect(la), AF.Copy))
 
-    op("g", lambda: g.iota(T.vw[:, C * me:C * me + C], [[0, C]], -4096, 0, **flag))
     k_vl = op("g", lambda: g.iota(T.vl[:], [[0, C]], 0, 0, **flag))
 
     dma("y", "d_tr", T.tr[112:128, :], T.to[:])
     tr = dma("y", "d_tr", T.tr[0:112, :], T.lr[:], own, ("a_raw", 6 * len(raw)))
 
-    def lin(out, a, b, scale, bias):
-        return op("s", lambda: S.activation(out[:, a:b], T.ic[:, a:b], AF.Identity, bias=float(bias), scale=float(scale)),
-                  k_ic)
-
-    lin(T.qc, 0, me + 1, 1, 3 - me)
+    k_pos = op("s", lambda: S.activation(T.pos[:], T.ic[:], AF.Identity, bias=pr), k_tdd)
     if me < N - 1:
-        lin(T.qc, me + 1, N, 1, 3 - me - N)
         lin(T.ba, me + 1, N, -P1, 48 - P1 + P1 * (me + N))
     if me > 0:
         lin(T.ba, 0, me, -P1, 48 - P1 + P1 * me)
-    lin(T.ba, me, me + 1, 0, 0)
-    op("s", lambda: S.activation(T.pos[:, 0:16], T.ic[:], AF.Identity, bias=pr), k_td3)
-    k_pos = op("s", lambda: S.activation(T.pos[:, 16:32], T.ic[:], AF.Identity, bias=pr))
-    k_zr = lin(T.zr, 0, N, 1, 12 - me)
+    k_ba = lin(T.ba, me, me + 1, 0, 0)
+    k_vw = op("s", lambda: S.activation(T.vw[:, C * me:C * me + C], T.rst[:], AF.Identity, bias=-4096.0, scale=0.0),
+              k_mem)
 
-    k_r7 = op("v", lambda: V.memset(T.rst7[:], 1.0))
-    k_r7 = op("v", lambda: V.memset(T.rst7[:, 0:224:7], 0.0), k_r7)
-    k_wme = op("v", lambda: V.tensor_scalar(T.wme[:], T.ic[:], float(me), None, A.is_equal))
-    k_dup = op("v", lambda: V.tensor_copy(T.dup[:], T.jf[:]))
     bb, nn = T.cb[:, 0:4 * N:4], T.cb[:, 1:4 * N:4]
     cn = ("a_cnt", 6 * len(eng))
-    k_ci = op("v", lambda: V.tensor_scalar(T.c7i[:, 0:N], nn, 3.0, 1.0 / 7, A.add, A.mult), cn, k_nm)
-    k_q = op("v", lambda: V.tensor_tensor(T.qa[:, 0:N], bb, T.qc[:, 0:N], A.add), k_pos)
-    k_c7 = op("v", lambda: V.tensor_copy(T.c7[:, 0:N], T.c7i[:, 0:N]), k_ci)
+    k_c7 = op("v", lambda: V.tensor_scalar(T.c7[:, 0:N], nn, R23, None, A.add), cn, k_nm)
+    k_q = op("v", lambda: V.tensor_tensor(T.qa[:, 0:N], bb, T.qc[:, 0:N], A.add), k_qc, k_b)
+    k_rx = op("v", lambda: V.tensor_tensor_scan(T.zz[:, rx + 1:rx + 8], T.c7[:, 0:N], T.mg[:, 0:N], 0.0, A.add, A.add),
+              k_c7, k_mg, k_zz)
     k_qi = op("v", lambda: V.tensor_scalar(T.qi[:, 0:N], T.qa[:, 0:N], 1.0 / 7, None, A.mult), k_q)
-    k_rx = op("v", lambda: V.tensor_tensor_scan(T.rx[:, 1:8], T.c7[:, 0:N], T.c7[:, 0:N], 0.0, A.add, A.max), k_c7)
-    k_aa = op("v", lambda: V.tensor_tensor(T.aa[:, 0:N], T.qi[:, 0:N], T.ba[:, 0:N], A.add), k_qi)
-    k_a = op("v", lambda: V.tensor_tensor(T.aj[:, 1:8], T.aa[:, 0:N], T.rx[:, 0:N], A.subtract), k_rx, k_aa)
-    k_jj = op("v", lambda: V.tensor_tensor(T.jj[:, 0:N], T.aj[:, 1:8], T.aj[:, 0:N], A.subtract), k_a)
-    ka = op("v", lambda: V.tensor_scalar(T.trd[:], T.tr[:], 8, None, A.arith_shift_right), tr)
-    kb = op("v", lambda: V.tensor_copy(T.tr16[:], T.tr[:]))
-    k_t3 = op("v", lambda: V.tensor_copy(T.trd16[:], T.trd[:]), ka)
+    k_aa = op("v", lambda: V.tensor_tensor(T.aa[:, 0:N], T.qi[:, 0:N], T.ba[:, 0:N], A.add), k_qi, k_ba)
+    kb = op("v", lambda: V.tensor_copy(T.tr16[:], T.tr[:]), tr)
+    k_a = op("v", lambda: V.tensor_tensor(T.zz[:, aj + 1:aj + 8], T.aa[:, 0:N], T.zz[:, rx:rx + N], A.subtract),
+             k_rx, k_aa)
+    k_t3 = op("v", lambda: V.tensor_scalar(T.trd16[:], T.tr[:], -127.5, 1.0 / C, A.add, A.mult))
+    k_jj = op("v", lambda: V.tensor_tensor(T.jj[:, 0:N], T.zz[:, aj + 1:aj + 8], T.zz[:, aj:aj + N], A.subtract), k_a)
     k_mk3 = op("s", lambda: S.activation(T.mk3[:], T.wme[:].indirect(T.trd16[:]), AF.Copy), k_t3, k_wme)
-    k_gr = op("v", lambda: V.tensor_scalar(T.gr[:, 0:224:7], T.pos[:], T.jj[:, 0:1], None, A.add), k_jj)
+    k_zr = lin(T.zr, 0, N, 1, 12 - me)
+    k_gr = op("v", lambda: V.tensor_scalar(T.gr[:, 0:224:7], T.pos[:], T.jj[:, 0:1], None, A.add), k_jj, k_pos)
     for r in range(1, N):
-        k_gr = op("v", lambda: V.tensor_scalar(T.gr[:, r:224:7], T.pos[:], T.rx[:, r:r + 1], T.jj[:, r:r + 1],
+        k_gr = op("v", lambda: V.tensor_scalar(T.gr[:, r:224:7], T.pos[:], T.zz[:, rx + r:rx + r + 1], T.jj[:, r:r + 1],
                                                A.is_ge, A.mult))
     k = op("v", lambda: V.tensor_tensor_scan(T.gs[:], T.rst7[:], T.gr[:], 0.0, A.mult, A.add), k_gr, k_r7)
     k = op("v", lambda: V.transpose(T.l2t[:], T.gs[:, 6:224:7]), k)
@@ -238,7 +242,7 @@ def rank_program(g, core, T, topo):
     k_l2 = op("v", lambda: V.tensor_scalar(T.lst2[:, e:21], T.l2t[:, 0:3 * (me + 1)], float(L1W - 1), None, A.min), k)
 
     k = op("v", lambda: V.tensor_tensor_scan(T.kv[:], T.mk3[:], T.mk3[:], 0.0, A.add, A.max), k_mk3)
-    k_v = op("v", lambda: V.tensor_copy(T.vw[:].indirect(T.tr16[:]), T.kv[:]), k, kb, k_vl)
+    k_v = op("v", lambda: V.tensor_copy(T.vw[:].indirect(T.tr16[:]), T.kv[:]), k, kb, k_vw)
     for i in range(4):
         vl = dma("y", "d_vl", T.vl[32 * i:32 * i + 4 * N:4, :], T.vw[0:16 * N:16, C * me:C * me + C], k_v, k_vl)
 
@@ -256,11 +260,11 @@ def rank_program(g, core, T, topo):
     to_each([T.out2s[:, a:a + P2] for a in blk], [T.land2s[:, a:a + P2] for a in lnd], two, "a_s2", "l_s2")
     k_a2 = op("v", lambda: V.tensor_copy(T.land2q[:, 6 * S2:7 * S2].bitcast(u32),
                                          T.land1q[:].bitcast(u32).indirect(la)))
-    k_b2 = op("s", lambda: S.activation(T.land2s[:, 6 * S2:7 * S2], T.land1s[:].indirect(la), AF.Copy))
     k_f1 = op("v", lambda: V.tensor_tensor(T.f1[:, 0:N], bb, T.zr[:, 0:N], A.add), k_zr)
-    k_f2 = op("v", lambda: V.tensor_scalar(T.f2[:, 0:N], T.rx[:, 0:N], 7.0 * U, -1.0 * U, A.mult, A.add))
-    k_f = op("v", lambda: V.tensor_tensor(T.fp[:, 0:4 * N:4], T.f1[:, 0:N], T.f2[:, 0:N], A.add), k_f2)
-    k_ft = op("v", lambda: V.transpose(T.ft[:], T.fp[:]), k_f)
+    k_f2 = op("v", lambda: V.tensor_scalar(T.f2[:, 0:N], T.zz[:, rx:rx + N], 7.0 * U, -1.0 * U, A.mult, A.add))
+    k_f = op("v", lambda: V.tensor_tensor(T.zz[:, 0:4 * N:4], T.f1[:, 0:N], T.f2[:, 0:N], A.add), k_f2)
+    k_dup = op("v", lambda: V.tensor_copy(T.dup[:], T.jf[:, 0:32]))
+    k_ft = op("v", lambda: V.transpose(T.ft[:], fp), k_f)
     k_wq = op("v", lambda: V.quantize_mx(T.wq[:], T.ws[:], T.wt[:]), wl)
 
     for i in range(2):
@@ -268,6 +272,7 @@ def rank_program(g, core, T, topo):
         k = op("s", lambda: S.activation(T.w3[:, h], T.vl[:].indirect(T.dup[:, 16 * i:16 * i + 16]), AF.Relu,
                                          bias=T.ft[:, 3 * me:3 * me + 1], scale=float(U + 1)), vl, k_ft, k_dup)
         k = op("v", lambda: V.transpose(T.y3[:, h], T.w3[:, h]), k)
+    k_b2 = op("s", lambda: S.activation(T.land2s[:, 6 * S2:7 * S2], T.land1s[:].indirect(la), AF.Copy))
     k = op("v", lambda: V.tensor_tensor(T.fa[:], T.y3[:, 0:512:8], T.y3[:, 4:512:8], A.add), k)
     k = op("v", lambda: V.tensor_tensor(T.fb[:], T.fa[:, 0:64:2], T.fa[:, 1:64:2], A.add), k)
     k = op("v", lambda: V.tensor_tensor(T.pk[:], T.fb[:, 0:32:2], T.fb[:, 1:32:2], A.add), k)

from concourse.bass import DstId, RemoteDMATransfer
from concourse.mybir import dt, AluOpType, ActivationFunctionType

N, C = 7, 256
P1, P2, S2 = 37, 42, 48
L1W = 48 + 6 * P1
U = 1024
CA = 352
R23 = 12582912.0

F32, BF, I32, U16, CODES, PLANE = "float32", "bfloat16", "int32", "uint16", "float8_e4m3fn_x4", "uint8"
SCRATCH = {
    "ta": ("sbuf", [128, 33], F32), "td3": ("sbuf", [128, 32], F32),
    "tb": ("sbuf", [128, 65], F32), "tdb": ("sbuf", [128, 64], F32), "tdc": ("sbuf", [128, 32], F32),
    "ic": ("sbuf", [128, 32], F32), "win": ("sbuf", [128, 16], BF), "win2": ("sbuf", [128, 16], BF),
    "wme": ("sbuf", [128, 16], BF), "rst": ("sbuf", [128, C], BF), "rst7": ("sbuf", [128, 7 * 32], F32),
    "cv": ("sbuf", [128, 128], F32), "cvb": ("sbuf", [128, 128], BF),
    "ji": ("sbuf", [128, 34], F32), "jm": ("sbuf", [128, 34], I32), "jf": ("sbuf", [128, 34], F32),
    "ja": ("sbuf", [128, 34], F32), "jb": ("sbuf", [128, 34], F32), "jc": ("sbuf", [128, 34], F32),
    "sig": ("sbuf", [128, 34], U16), "dup": ("sbuf", [128, 32], U16), "pos": ("sbuf", [128, 32], F32),
    "qc": ("sbuf", [128, 8], F32), "ba": ("sbuf", [128, 8], F32), "zr": ("sbuf", [128, 8], F32),
    "mg": ("sbuf", [128, 8], F32),
    "tw": ("sbuf", [128, 16], I32), "td16": ("sbuf", [128, 16], U16),
    "mk": ("sbuf", [128, C], BF), "jk": ("sbuf", [128, C], BF), "jn": ("sbuf", [128, C], F32),
    "dm": ("sbuf", [128, C], BF), "cc": ("sbuf", [128, C], BF),
    "xx": ("sbuf", [128, C], BF), "xc": ("sbuf", [128, C], BF),
    "s16": ("sbuf", [128, 8], U16), "inv": ("sbuf", [128, 272], BF), "gg": ("sbuf", [128, 544], BF),
    "yy": ("sbuf", [128, 544], BF), "lf": ("sbuf", [128, 18], F32), "lst1": ("sbuf", [128, 18], U16),
    "cb": ("sbuf", [128, 4 * N], F32), "c7": ("sbuf", [128, 8], F32),
    "zz": ("sbuf", [128, 48], F32),
    "qa": ("sbuf", [128, 8], F32), "qi": ("sbuf", [128, 8], I32),
    "aa": ("sbuf", [128, 8], F32), "jj": ("sbuf", [128, 8], F32),
    "gr": ("sbuf", [128, 7 * 32], F32), "gs": ("sbuf", [128, 7 * 32], F32),
    "l2t": ("sbuf", [128, 32], F32), "lst2": ("sbuf", [128, 22], U16),
    "rd": ("dram", [128, 2], I32), "lr": ("dram", [N, 128, 2], I32),
    "tr": ("sbuf", [128, 16], I32), "tr16": ("sbuf", [128, 16], U16),
    "trd16": ("sbuf", [128, 16], U16), "mk3": ("sbuf", [128, C], BF), "kv": ("sbuf", [128, C], BF),
    "vw": ("sbuf", [128, N * C], BF), "vl": ("sbuf", [128, C], BF),
    "f1": ("sbuf", [128, 8], F32), "f2": ("sbuf", [128, 8], F32),
    "ft": ("sbuf", [128, 32], F32), "w3": ("sbuf", [128, 512], F32), "y3": ("sbuf", [128, 512], F32),
    "fa": ("sbuf", [128, 64], F32), "fb": ("sbuf", [128, 32], F32), "pk": ("sbuf", [128, 16], I32),
    "ql": ("sbuf", [128, 16], I32), "qh": ("sbuf", [128, 16], I32), "qq": ("sbuf", [128, 16], I32),
    "ua": ("sbuf", [128, 16], F32), "ub": ("sbuf", [128, 16], F32),
    "uc": ("sbuf", [128, 16], F32), "ud": ("sbuf", [128, 16], F32), "lst3": ("sbuf", [128, 16], U16),
    "xt": ("sbuf", [128, 4 * C], BF), "wt": ("sbuf", [128, 512], BF),
    "xq": ("sbuf", [128, C], CODES), "xs": ("sbuf", [128, C], PLANE),
    "wq": ("sbuf", [128, 128], CODES), "ws": ("sbuf", [128, 128], PLANE),
    "out1q": ("sbuf", [128, 240], CODES), "out1s": ("sbuf", [128, 240], PLANE),
    "land1q": ("sbuf", [128, L1W], CODES), "land1s": ("sbuf", [128, L1W], PLANE),
    "out2q": ("sbuf", [128, 6 * S2], CODES), "out2s": ("sbuf", [128, 6 * S2], PLANE),
    "land2q": ("sbuf", [128, 7 * S2], CODES), "land2s": ("sbuf", [128, 7 * S2], PLANE),
    "fq": ("sbuf", [128, C], CODES), "fs": ("sbuf", [128, C], PLANE),
    "ps": ("psum", [128, 1024], F32), "ys": ("sbuf", [128, C], F32),
}
SEMAPHORES = ["ev", "es", "eg", "et",
              "d_rd", "d_tw", "d_x", "d_w", "d_own", "d_tr", "d_vl", "d_y0", "d_y1",
              "a_raw", "a_cnt", "a_c1", "a_s1", "a_c2", "a_s2",
              "l_raw", "l_cnt", "l_c1", "l_s1", "l_c2", "l_s2"]


def rank_program(g, core, T, topo):
    me = T.rank_of(core)
    if me is None:
        return
    A, AF = AluOpType, ActivationFunctionType
    queue = {"v": g.vector, "s": g.scalar, "g": g, "t": g.tensor, "y": g.sync}
    count = {}
    seen = {k: {} for k in queue}

    def wait(q, *deps):
        for sem, n in deps:
            if seen[q].get(sem, 0) < n:
                queue[q].wait_ge(T.sem[sem], n)
                seen[q][sem] = n

    def op(q, call, *deps):
        wait(q, *deps)
        sem = "e" + q
        call().then_inc(T.sem[sem], 1)
        count[sem] = count.get(sem, 0) + 1
        return (sem, count[sem])

    def dma(q, sem, out, in_, *deps):
        wait(q, *deps)
        queue[q].dma_start(out, in_).then_inc(T.sem[sem], 16)
        count[sem] = count.get(sem, 0) + 16
        return (sem, count[sem])

    V, S = g.vector, g.scalar

    peers = [T.cores[(me + 1 + x) % N] for x in range(N - 1)]
    eng = [e for e in topo.engines(core, peers[0]) if all(e in topo.engines(core, p) for p in peers)]
    ev, od = eng[0::2], eng[1::2]

    def mask(es):
        return sum(1 << e for e in es)

    one = [[e] for e in ev] + [od[0:2], od[2:4]]
    two = [ev[0:2], ev[2:4]] + [[e] for e in od]

    def dst(p):
        rid, pid, _ = topo.addr(p)
        return DstId(rid=rid, pnc=pid)

    def to_all(src, d, es, remote, local):
        g.remote_dma_fused([RemoteDMATransfer(dst_ids=[dst(p) for p in peers], dma_engine_mask=mask(es),
                                              remote_sem=T.sem[remote], srcs=[src], dsts=[d] * len(peers))],
                           local_sem=T.sem[local])

    def to_each(srcs, dsts, masks, remote, local):
        g.remote_dma_fused([RemoteDMATransfer(dst_ids=[dst(p)], dma_engine_mask=mask(m), remote_sem=T.sem[remote],
                                              src=s, dst=d) for p, s, d, m in zip(peers, srcs, dsts, masks)],
                           local_sem=T.sem[local])

    rd = dma("y", "d_rd", T.rd[:], T.to[:])
    for i in range(8):
        tw = dma("sy"[i % 2], "d_tw", T.tw[16 * i:16 * i + 16, :], T.to[:])
    xl = dma("y", "d_x", T.xt[:], T.x[:])
    own = dma("s", "d_own", T.lr[me], T.to[:])
    wl = dma("s", "d_w", T.wt[:], T.w[:])

    flag = dict(allow_small_or_imprecise_dtypes=True)
    k_ta = op("g", lambda: g.iota(T.ta[:], [[1, 11], [0, 3]], 0, 0, **flag))
    k_ic = op("g", lambda: g.iota(T.ic[:], [[0, 2], [1, 16]], 0, 0, **flag))
    k_ji = op("g", lambda: g.iota(T.ji[:], [[16, 17], [0, 2]], 0, 0, **flag))
    k_tb = op("g", lambda: g.iota(T.tb[:, 0:32], [[16, 2], [0, 16]], 0, 0, **flag))
    k_cv = op("g", lambda: g.iota(T.cv[:], [[32, 8], [1, 16]], 0, 0, **flag))
    wait("g", rd)
    raw = eng[:1]
    to_all(T.rd[:], T.lr[me], raw, "a_raw", "l_raw")
    k_tc = op("g", lambda: g.iota(T.tb[:, 32:65], [[0, 11], [16, 3]], 0, 0, **flag))

    op("v", lambda: V.memset(T.dm[:, 0:1], -255.0))
    k_rst = op("v", lambda: V.memset(T.rst[:], 1.0))
    k_inv = op("v", lambda: V.memset(T.inv[:], 0.0))
    k_td3 = op("v", lambda: V.transpose(T.td3[:], T.ta[:, 0:32]), k_ta)
    k_mem = op("v", lambda: V.memset(T.rst[:, 0:C:32], 0.0), k_rst)
    pd, p15, odd, pr = T.td3[:, 0:1], T.tdc[:, 0:1], T.tdb[:, 0:1], T.tdb[:, 32:33]
    k_win2 = op("v", lambda: V.tensor_scalar(T.win2[:], T.ic[:, 0:16], pd, None, A.is_lt), k_td3, k_ic)
    k_win = op("v", lambda: V.tensor_scalar(T.win[:], T.ic[:, 0:16], pd, 256.0, A.is_equal, A.mult))
    k_tdc = op("v", lambda: V.transpose(T.tdc[:], T.ic[:]))
    k_wme = op("v", lambda: V.tensor_scalar(T.wme[:], T.ic[:, 0:16], float(me), None, A.is_equal))
    k_tdb = op("v", lambda: V.transpose(T.tdb[:, 0:32], T.tb[:, 0:32]), k_tb)
    k_jf = op("s", lambda: S.activation(T.jf[:], T.ji[:], AF.Identity, bias=p15), k_tdc, k_ji)
    k_jm = op("v", lambda: V.tensor_scalar(T.jm[:], T.jf[:], -18.0, 1.0 / P1, A.add, A.mult), k_jf)
    k_ja = op("s", lambda: S.activation(T.ja[:], T.jf[:], AF.Identity, bias=1.0, scale=7.0), k_jf)

    k_td = op("v", lambda: V.tensor_scalar(T.td16[:], T.tw[:], -127.5, 1.0 / C, A.add, A.mult), tw)
    bm, nm = T.cb[:, 4 * me:4 * me + 1], T.cb[:, 4 * me + 1:4 * me + 2]
    k_b = op("s", lambda: S.activation(T.jk[:], T.win2[:].indirect(T.td16[:]), AF.Identity, accum_out=bm), k_td, k_win2)
    k_jb = op("v", lambda: V.tensor_scalar(T.jb[:], T.jm[:], float(1 - 7 * P1), None, A.mult), k_jm)
    k_mk = op("v", lambda: V.tensor_copy(T.mk[:], T.win[:].indirect(T.td16[:])), k_td, k_win)
    k_nm = op("s", lambda: S.activation(T.jn[:], T.mk[:], AF.Identity, bias=3.0 / 7 / C, scale=1.0 / 7 / 256,
                                        accum_out=nm), k_mk)
    k_jc = op("v", lambda: V.tensor_tensor(T.jc[:], T.ja[:], T.jb[:], A.add), k_jb, k_ja)
    k_dm = op("v", lambda: V.tensor_scalar(T.dm[:, 1:C], T.mk[:, 0:C - 1], -255.0 / 256, None, A.mult), k_mk)
    k_sig = op("v", lambda: V.tensor_copy(T.sig[:], T.jc[:]), k_jc)
    k_cc = op("v", lambda: V.tensor_tensor_scan(T.cc[:], T.mk[:], T.dm[:], bm, A.add, A.add), k_dm, k_b)
    k_xx = op("v", lambda: V.transpose(T.xx[:], T.cc[:]), k_cc)
    k_xc = op("v", lambda: V.tensor_tensor_scan(T.xc[:], T.rst[:], T.xx[:], 0.0, A.mult, A.max), k_xx, k_mem)
    k_s = op("v", lambda: V.tensor_copy(T.s16[:], T.xc[:, 31:C:32]), k_xc)
    k_cvb = op("s", lambda: S.activation(T.cvb[:], T.cv[:], AF.Identity, bias=odd), k_cv, k_tdb)
    k_sc = op("v", lambda: V.tensor_copy(T.inv[:].indirect(T.s16[:]), T.cvb[:]), k_s, k_cvb, k_inv)

    def lin(out, a, b, scale, bias):
        return op("s", lambda: S.activation(out[:, a:b], T.ic[:, a:b], AF.Identity, bias=float(bias), scale=float(scale)),
                  k_ic)

    fp, rx, aj = T.zz[:, 0:32], 32, 40
    k_zz = op("s", lambda: S.activation(T.zz[:], T.cv[:, 0:48], AF.Copy, scale=0.0))
    k_mg = lin(T.mg, 0, 8, 0, -R23)
    op("s", lambda: S.activation(T.rst7[:, 0:128], T.cv[:], AF.Identity, bias=1.0, scale=0.0))
    k_r7 = op("s", lambda: S.activation(T.rst7[:, 128:224], T.cv[:, 0:96], AF.Identity, bias=1.0, scale=0.0))
    k_r7 = op("s", lambda: S.activation(T.rst7[:, 0:224:7], T.cv[:, 0:32], AF.Copy, scale=0.0), k_r7)

    k_ga = op("s", lambda: S.activation(T.gg[:, 0:CA], T.inv[:].indirect(T.sig[:, 0:CA // 16]), AF.Copy), k_sc, k_sig)
    k_gb = op("v", lambda: V.tensor_copy(T.gg[:, CA:544], T.inv[:].indirect(T.sig[:, CA // 16:34])), k_sc, k_sig)
    k_xq = op("v", lambda: V.quantize_mx(T.xq[:], T.xs[:], T.xt[:]), xl)
    k_yy = op("v", lambda: V.transpose(T.yy[:], T.gg[:]), k_ga, k_gb)
    k_lf = op("v", lambda: V.tensor_tensor(T.lf[:, 0:17], T.yy[:, 0:544:32], T.yy[:, 16:544:32], A.add), k_yy)
    k_l1 = op("v", lambda: V.tensor_copy(T.lst1[:, 0:17], T.lf[:, 0:17]), k_lf)
    k_qc = lin(T.qc, 0, me + 1, 1, 3 - me)
    if me < N - 1:
        k_qc = lin(T.qc, me + 1, N, 1, 3 - me - N)

    wait("g", k_nm)
    to_all(T.cb[:, 4 * me:4 * me + 2], T.cb[:, 4 * me:4 * me + 2], eng, "a_cnt", "l_cnt")

    lo, la = T.lst1[:, 2:17], T.lst1[:, 0:3]
    u32, u8 = dt.uint32, dt.uint8
    k_p1 = op("v", lambda: V.tensor_copy(T.out1q[:].bitcast(u32), T.xq[:].bitcast(u32).indirect(lo)), k_l1, k_xq)
    k_o1 = op("s", lambda: S.activation(T.out1s[:], T.xs[:].indirect(lo), AF.Copy), k_l1, k_xq)
    wait("g", k_p1)
    blk = [P1 * (x + 1) - 32 for x in range(N - 1)]
    lnd = [48 + P1 * x for x in range(N - 1)]
    to_each([T.out1q[:, a:a + P1].bitcast(u8) for a in blk], [T.land1q[:, a:a + P1].bitcast(u8) for a in lnd], one,
            "a_c1", "l_c1")
    wait("g", k_o1)
    to_each([T.out1s[:, a:a + P1] for a in blk], [T.land1s[:, a:a + P1] for a in lnd], two, "a_s1", "l_s1")
    k_a1 = op("v", lambda: V.tensor_copy(T.land1q[:, 0:48].bitcast(u32), T.xq[:].bitcast(u32).indirect(la)))
    k_tdd = op("v", lambda: V.transpose(T.tdb[:, 32:64], T.tb[:, 32:64]), k_tc)
    k_b1 = op("s", lambda: S.activation(T.land1s[:, 0:48], T.xs[:].indirect(la), AF.Copy))

    k_vl = op("g", lambda: g.iota(T.vl[:], [[0, C]], 0, 0, **flag))

    dma("y", "d_tr", T.tr[112:128, :], T.to[:])
    tr = dma("y", "d_tr", T.tr[0:112, :], T.lr[:], own, ("a_raw", 6 * len(raw)))

    k_pos = op("s", lambda: S.activation(T.pos[:], T.ic[:], AF.Identity, bias=pr), k_tdd)
    if me < N - 1:
        lin(T.ba, me + 1, N, -P1, 48 - P1 + P1 * (me + N))
    if me > 0:
        lin(T.ba, 0, me, -P1, 48 - P1 + P1 * me)
    k_ba = lin(T.ba, me, me + 1, 0, 0)
    k_vw = op("s", lambda: S.activation(T.vw[:, C * me:C * me + C], T.rst[:], AF.Identity, bias=-4096.0, scale=0.0),
              k_mem)

    bb, nn = T.cb[:, 0:4 * N:4], T.cb[:, 1:4 * N:4]
    cn = ("a_cnt", 6 * len(eng))
    k_c7 = op("v", lambda: V.tensor_scalar(T.c7[:, 0:N], nn, R23, None, A.add), cn, k_nm)
    k_q = op("v", lambda: V.tensor_tensor(T.qa[:, 0:N], bb, T.qc[:, 0:N], A.add), k_qc, k_b)
    k_rx = op("v", lambda: V.tensor_tensor_scan(T.zz[:, rx + 1:rx + 8], T.c7[:, 0:N], T.mg[:, 0:N], 0.0, A.add, A.add),
              k_c7, k_mg, k_zz)
    k_qi = op("v", lambda: V.tensor_scalar(T.qi[:, 0:N], T.qa[:, 0:N], 1.0 / 7, None, A.mult), k_q)
    k_aa = op("v", lambda: V.tensor_tensor(T.aa[:, 0:N], T.qi[:, 0:N], T.ba[:, 0:N], A.add), k_qi, k_ba)
    kb = op("v", lambda: V.tensor_copy(T.tr16[:], T.tr[:]), tr)
    k_a = op("v", lambda: V.tensor_tensor(T.zz[:, aj + 1:aj + 8], T.aa[:, 0:N], T.zz[:, rx:rx + N], A.subtract),
             k_rx, k_aa)
    k_t3 = op("v", lambda: V.tensor_scalar(T.trd16[:], T.tr[:], -127.5, 1.0 / C, A.add, A.mult))
    k_jj = op("v", lambda: V.tensor_tensor(T.jj[:, 0:N], T.zz[:, aj + 1:aj + 8], T.zz[:, aj:aj + N], A.subtract), k_a)
    k_mk3 = op("s", lambda: S.activation(T.mk3[:], T.wme[:].indirect(T.trd16[:]), AF.Copy), k_t3, k_wme)
    k_zr = lin(T.zr, 0, N, 1, 12 - me)
    k_gr = op("v", lambda: V.tensor_scalar(T.gr[:, 0:224:7], T.pos[:], T.jj[:, 0:1], None, A.add), k_jj, k_pos)
    for r in range(1, N):
        k_gr = op("v", lambda: V.tensor_scalar(T.gr[:, r:224:7], T.pos[:], T.zz[:, rx + r:rx + r + 1], T.jj[:, r:r + 1],
                                               A.is_ge, A.mult))
    k = op("v", lambda: V.tensor_tensor_scan(T.gs[:], T.rst7[:], T.gr[:], 0.0, A.mult, A.add), k_gr, k_r7)
    k = op("v", lambda: V.transpose(T.l2t[:], T.gs[:, 6:224:7]), k)
    e = 3 * (N - 1 - me)
    if e:
        op("v", lambda: V.tensor_scalar(T.lst2[:, 0:e], T.l2t[:, 3 * (me + 1):21], float(L1W - 1), None, A.min), k)
    k_l2 = op("v", lambda: V.tensor_scalar(T.lst2[:, e:21], T.l2t[:, 0:3 * (me + 1)], float(L1W - 1), None, A.min), k)

    k = op("v", lambda: V.tensor_tensor_scan(T.kv[:], T.mk3[:], T.mk3[:], 0.0, A.add, A.max), k_mk3)
    k_v = op("v", lambda: V.tensor_copy(T.vw[:].indirect(T.tr16[:]), T.kv[:]), k, kb, k_vw)
    for i in range(4):
        vl = dma("y", "d_vl", T.vl[32 * i:32 * i + 4 * N:4, :], T.vw[0:16 * N:16, C * me:C * me + C], k_v, k_vl)

    lo, la = T.lst2[:, 0:18], T.lst2[:, 18:21]
    c1, s1 = ("a_c1", 8), ("a_s1", 8)
    k_p2 = op("v", lambda: V.tensor_copy(T.out2q[:].bitcast(u32), T.land1q[:].bitcast(u32).indirect(lo)),
              k_l2, k_a1, c1)
    k_o2 = op("s", lambda: S.activation(T.out2s[:], T.land1s[:].indirect(lo), AF.Copy), k_l2, k_b1, s1)
    wait("g", k_p2)
    blk = [S2 * x for x in range(N - 1)]
    lnd = [S2 * (N - 2 - x) for x in range(N - 1)]
    to_each([T.out2q[:, a:a + P2].bitcast(u8) for a in blk], [T.land2q[:, a:a + P2].bitcast(u8) for a in lnd], one,
            "a_c2", "l_c2")
    wait("g", k_o2)
    to_each([T.out2s[:, a:a + P2] for a in blk], [T.land2s[:, a:a + P2] for a in lnd], two, "a_s2", "l_s2")
    k_a2 = op("v", lambda: V.tensor_copy(T.land2q[:, 6 * S2:7 * S2].bitcast(u32),
                                         T.land1q[:].bitcast(u32).indirect(la)))
    k_f1 = op("v", lambda: V.tensor_tensor(T.f1[:, 0:N], bb, T.zr[:, 0:N], A.add), k_zr)
    k_f2 = op("v", lambda: V.tensor_scalar(T.f2[:, 0:N], T.zz[:, rx:rx + N], 7.0 * U, -1.0 * U, A.mult, A.add))
    k_f = op("v", lambda: V.tensor_tensor(T.zz[:, 0:4 * N:4], T.f1[:, 0:N], T.f2[:, 0:N], A.add), k_f2)
    k_dup = op("v", lambda: V.tensor_copy(T.dup[:], T.jf[:, 0:32]))
    k_ft = op("v", lambda: V.transpose(T.ft[:], fp), k_f)
    k_wq = op("v", lambda: V.quantize_mx(T.wq[:], T.ws[:], T.wt[:]), wl)

    for i in range(2):
        h = slice(256 * i, 256 * i + 256)
        k = op("s", lambda: S.activation(T.w3[:, h], T.vl[:].indirect(T.dup[:, 16 * i:16 * i + 16]), AF.Relu,
                                         bias=T.ft[:, 3 * me:3 * me + 1], scale=float(U + 1)), vl, k_ft, k_dup)
        k = op("v", lambda: V.transpose(T.y3[:, h], T.w3[:, h]), k)
    k_b2 = op("s", lambda: S.activation(T.land2s[:, 6 * S2:7 * S2], T.land1s[:].indirect(la), AF.Copy))
    k = op("v", lambda: V.tensor_tensor(T.fa[:], T.y3[:, 0:512:8], T.y3[:, 4:512:8], A.add), k)
    k = op("v", lambda: V.tensor_tensor(T.fb[:], T.fa[:, 0:64:2], T.fa[:, 1:64:2], A.add), k)
    k = op("v", lambda: V.tensor_tensor(T.pk[:], T.fb[:, 0:32:2], T.fb[:, 1:32:2], A.add), k)
    kl = op("v", lambda: V.tensor_scalar(T.ql[:], T.pk[:], U - 1, None, A.bitwise_and), k)
    kh = op("v", lambda: V.tensor_scalar(T.qh[:], T.pk[:], 0.5 - 3.5 * U, 1.0 / (7 * U), A.add, A.mult))
    kq = op("v", lambda: V.tensor_scalar(T.qq[:], T.ql[:], -3.0, 1.0 / 7, A.add, A.mult), kl)
    ka = op("v", lambda: V.tensor_scalar(T.ua[:], T.ql[:], float(S2), None, A.mult))
    kb = op("v", lambda: V.tensor_scalar(T.ub[:], T.qq[:], -7.0 * S2, None, A.mult), kq)
    kc = op("v", lambda: V.tensor_tensor(T.uc[:], T.ua[:], T.qh[:], A.add), ka, kh)
    kd = op("v", lambda: V.tensor_tensor(T.ud[:], T.ub[:], T.uc[:], A.add), kb, kc)
    k_l3 = op("v", lambda: V.tensor_copy(T.lst3[:], T.ud[:]), kd)

    c2, s2 = ("a_c2", 8), ("a_s2", 8)
    cols = [slice(128 * i, 128 * i + 128) for i in range(2)]
    lst = [T.lst3[:, 8 * i:8 * i + 8] for i in range(2)]
    kq = [op("v", lambda: V.tensor_copy(T.fq[:, cols[i]].bitcast(u32), T.land2q[:].bitcast(u32).indirect(lst[i])),
             k_l3, k_a2, c2) for i in range(2)]
    ks = [op("s", lambda: S.activation(T.fs[:, cols[0]], T.land2s[:].indirect(lst[0]), AF.Copy), k_l3, k_b2, s2),
          op("v", lambda: V.tensor_copy(T.fs[:, cols[1]], T.land2s[:].indirect(lst[1])), k_b2, s2)]
    mm = [op("t", lambda: g.tensor.matmul_mx(T.ps[:, 512 * i:512 * i + 128], T.wq[:], T.ws[:], T.fq[:, cols[i]],
                                             T.fs[:, cols[i]], True, True), kq[i], ks[i], k_wq) for i in range(2)]
    k0 = op("s", lambda: S.activation(T.ys[:, 0:128], T.ps[:, 0:128], AF.Copy), mm[0])
    k1 = op("v", lambda: V.tensor_copy(T.ys[:, 128:256], T.ps[:, 512:640]), mm[1])
    y0 = dma("s", "d_y0", T.y[:, 0:128], T.ys[:, 0:128], k0)
    y1 = dma("y", "d_y1", T.y[:, 128:256], T.ys[:, 128:256], k1)

    wait("g", ("l_raw", len(raw)))
    for sem in ("l_cnt", "l_c1", "l_s1", "l_c2", "l_s2"):
        wait("g", (sem, len(eng)))
    wait("y", y0, y1, *[(s, count[s]) for s in ("ev", "es", "eg", "et")])
